import numpy as np, ml_dtypes
CORES = [5,29,101,125,133,157,229,253]
N = 8
BF = ml_dtypes.bfloat16
W, TU, RO, Q, S = 4096, 256, 4, 9, 16
HOPS = [4, 1]
BL = TU // len(HOPS)
def pack(x, l, w, k, h):
    return {"field": x.reshape(N, 128, W).astype(np.float32).astype(BF), "tube": np.ascontiguousarray(l.reshape(N, 128, TU)).astype(np.int32),
            "wt": w.reshape(N, 128, 1).astype(np.int32), "kn": k.reshape(N, 128, 1).astype(np.int32), "lim": np.ascontiguousarray(h.reshape(N, 128, RO)).astype(np.int32)}
def parts(rng):
    dark = rng.random((N, 8, 1, W)) < rng.choice(np.array([0.04, 0.08, 0.15]), (N, 8, 1, 1))
    x = np.where(dark, rng.integers(0, 64, (N, 8, 16, W), dtype=np.int16), rng.integers(48, 256, (N, 8, 16, W), dtype=np.int16))
    l = rng.integers(0, W, (N, 8, 16, TU)); w = rng.integers(0, 256, (N, 8, 16)); k = rng.integers(0, 256, (N, 8, 16))
    return x, l, w, k, rng.integers(16, 72, (N, 8, 16, RO))
def setup_inputs(rng):
    return pack(*parts(rng))
def setup_inputs_spread(rng):
    sh = rng.choice(np.array([0, 0, 0, 0, 0, 1, 1, 2, 4, 8], np.int16), (N, 8, 1, W))
    x = rng.integers(0, 256, (N, 8, 16, W), dtype=np.int16) >> sh
    l = rng.integers(0, W, (N, 8, 16, TU)); l[:, 1::2] = np.minimum((W * rng.random((N, 4, 16, TU)) ** 3).astype(np.int64), W - 1)
    w = rng.integers(0, 256, (N, 8, 16)) >> rng.integers(0, 9, (N, 8, 16)); k = rng.integers(0, 256, (N, 8, 16)) >> rng.integers(0, 9, (N, 8, 16))
    h = rng.integers(0, 249, (N, 8, 16, RO)) >> rng.integers(0, 9, (N, 8, 1, RO))
    return pack(x, l, w, k, h)
def ends_of(rng, hi, shape):
    return np.where(rng.random(shape) < 0.14, rng.integers(0, hi + 1, shape), hi * rng.integers(0, 2, shape))
def setup_inputs_ends(rng):
    kind = rng.random((N, 8, 1, W)); top = np.int16(255)
    x = np.where(kind < 0.7, top, np.where(kind < 0.82, np.int16(0), top * rng.integers(0, 2, (N, 8, 16, W), dtype=np.int16)))
    i = np.arange(16)[:, None]
    b = ((np.arange(N)[:, None] + np.arange(8)[None, :]) & 1) * (W - 1)
    l = np.where(i < rng.integers(0, 17, (N, 8, 1, TU)), b[:, :, None, None], (W - 1) * rng.integers(0, 2, (N, 8, 16, TU)))
    free = ((np.arange(TU) * 5) & 15) < 5; l[..., free] = rng.integers(0, W, (N, 8, 16, int(np.count_nonzero(free))))
    w = ends_of(rng, 255, (N, 8, 16)); k = ends_of(rng, 255, (N, 8, 16))
    h = 248 * rng.integers(0, 2, (N, 8, 16, RO)); h[:, 1::2] = 248 * rng.integers(0, 2, (N, 4, 1, RO))
    for q in range(N):
        for g in range(8):
            o = W - 1 - b[q, g]; x[q, g][:, b[q, g]] = 255
            x[q, g][:, o] = 0 if (g & 3) < 2 or q == 1 else 255 * rng.integers(0, 2, 16) if (g & 3) == 2 else 255
    h[0, :, :, 0] = 0; h[0, 0, :, 1] = 248; h[1, :, :, 0] = 248; h[1, 0, :, 1] = 0; l[1, :, 15, :] = (W - 1 - b[1])[:, None]
    h[2, :, :, 0] = 0; h[2, 0, :, 0] = 248; l[2, 0] = b[2, 0]; l[2, 0, 15, :7] = W - 1 - b[2, 0]; h[2, :, :, 1] = 248
    p = N - 1; u = (15 * 65025) & 4095
    for g in range(4, 8):
        x[p, g][:, 0] = 255; x[p, g][:, W - 1] = 255; w[p, g] = 255
        if g == 5: w[p, g] = 0; w[p, g, 0] = 16; w[p, g, 1] = 1; x[p, g, 1, 0] = 15; x[p, g, 1, W - 1] = 15
        if g > 5:
            w[p, g, 0] = 0; k[p, g] = 255 * (np.arange(16) & 1)
            for j in (0, W - 1):
                x[p, g][:, ((u * u >> 4) + j) & (W - 1)] = 0
                x[p, g][:, ((u * u >> 4) + 255 * u + j) & (W - 1)] = 255 if g == 6 else 0
    return pack(x, l, w, k, h)
def setup_inputs_corners(rng):
    x, l, w, k, h = parts(rng); i = np.arange(16)[:, None]; v = np.arange(TU)
    for q in range(N):
        for g in range(8):
            c = (g + q) & 7
            if c == 0: h[q, g] = 0
            if c == 1: h[q, g] = 248; x[q, g] = np.minimum(x[q, g], 247)
            if c == 2:
                s = rng.integers(0, W, TU); s[0] = 0; s[1] = W - 1; l[q, g] = s[None, :]
            if c == 3:
                m = np.where(rng.random(W) < 0.9, Q, Q - 1)[None, :]
                x[q, g] = np.where(i < m, rng.integers(150, 256, (16, W)), rng.integers(0, 90, (16, W))); h[q, g] = 100
            if c == 4: w[q, g] = 0; k[q, g] = 0
            if c == 5:
                m = rng.random(W) < 0.9; x[q, g, 0, m] = 255; x[q, g, 1, m] = 15; w[q, g] = 0; w[q, g, 0] = 16; w[q, g, 1] = 1; k[q, g] = 255 * rng.integers(0, 2, 16)
            if c == 6:
                t = rng.integers(0, 4, (16, TU)); l[q, g] = np.where(t == 0, 0, np.where(t == 1, W - 1, np.where(t == 2, S * v, S * v + S - 1)))
            if c == 7:
                x[q, g][:, 0::2] = rng.integers(200, 256, (16, W // 2)); x[q, g][:, 1::2] = rng.integers(0, 64, (16, W // 2)); h[q, g] = 100
                l[q, g] = 2 * rng.integers(0, W // 2, (16, TU)) + (i == (v % 17)[None, :])
    return pack(x, l, w, k, h)
def setup_inputs_ties(rng):
    x, l, w, k, h = parts(rng)
    pr = 60 + 4 * rng.integers(0, 3, (N, 8, 16, 5)); x = np.take_along_axis(pr, np.broadcast_to(rng.integers(0, 5, (N, 8, 1, W)), (N, 8, 16, W)), 3)
    return pack(x, l, w, k, rng.integers(53, 66, (N, 8, 16, RO)))
def setup_inputs_brink(rng):
    x, l, w, k, h = parts(rng); r0 = int(rng.integers(0, 8)); v = np.arange(TU)
    h[..., 0] = 0; h[..., 1] = 248; h[..., 2:] = rng.integers(246, 249, (N, 8, 1, RO - 2))
    for g in range(8):
        c = (g + r0) & 7; low = rng.permutation(W)[:32]
        for q in range(N):
            if c < 4:
                o = rng.permutation(16); y = np.full((16, W), 254); y[o[:Q]] = 255
                b = np.nonzero(rng.random(W) < 0.1)[0]; y[o[rng.integers(0, Q, len(b))], b] = 254
                x[q, g] = y
            elif c < 6:
                x[q, g] = rng.integers(248, 256, (16, W)); x[q, g][:, low] = rng.integers(7, 9, (16, 32))
            else:
                x[q, g] = rng.integers(243, 256, (16, W)); x[q, g][:, low] = rng.integers(0, 4, (16, 32))
            if c >= 4:
                l[q, g, rng.integers(1, 16, TU), v] = low[rng.integers(0, 32, TU)]; h[q, g] = 0
            if c == 0:
                d = int(rng.integers(0, W)); s = rng.integers(0, W - 1, (16, TU)); l[q, g] = s + (s >= d)
                l[q, g, rng.integers(1, 16, 7), rng.permutation(TU)[:7]] = d
                x[q, g][:, d] = rng.integers(0, 248, 16); h[q, g, :, 0] = 248
    return pack(x, l, w, k, h)
def check_inputs(d):
    bad = []
    for a, lo, hi in (("field", 0, 255), ("tube", 0, W - 1), ("wt", 0, 255), ("kn", 0, 255), ("lim", 0, 248)):
        v = np.asarray(d[a]).astype(np.float64)
        if not (np.min(v) >= lo and np.max(v) <= hi): bad.append("range of " + a)
        elif np.any(v != np.floor(v)): bad.append("whole numbers of " + a)
    return bad
def reference(field, tube, wt, kn, lim):
    x = field.astype(np.float32).astype(np.int32).reshape(N, 8, 16, W)
    l = tube.astype(np.int64).reshape(N, 8, 16, TU)
    w = wt.astype(np.int64).reshape(N, 8, 16, 1); k = kn.astype(np.int64).reshape(N, 8, 16, 1); h = lim.astype(np.int64).reshape(N, 8, 16, RO)
    cut = [0] * N; v = np.arange(TU); j = np.arange(16)[:, None]
    for rnd in range(RO):
        if rnd: l = np.concatenate([np.roll(l[..., b * BL:(b + 1) * BL], HOPS[b], axis=0) for b in range(len(HOPS))], axis=-1)
        nl = np.zeros((N, 8, 16, TU), np.int64); nz = np.zeros((N, 8, 16, TU), np.int64); ncut = [0] * N
        for q in range(N):
            for g in range(8):
                X, L = x[q, g], l[q, g]
                M = np.minimum.accumulate(X[:, L], axis=1)
                holds = (M >= (h[q, g, :, rnd] + (cut[q] & 7))[:, None, None]).astype(np.int64)
                ok = (np.add.reduce(holds, axis=0) >= Q).astype(np.int64)
                m = np.maximum(np.add.reduce(ok, axis=0), 1) - 1
                Z = np.take_along_axis(M, np.broadcast_to(m[None, None, :], (16, 1, TU)), 1)[:, 0].astype(np.int64)
                u = np.add.reduce(w[q, g] * X[:, L[m, v]], axis=0) & 4095
                c = ((u * u >> 4)[None, :] + k[q, g] * u[None, :] + L) & (W - 1)
                s = np.add.reduce(np.abs(X[:, c] - Z[:, None, :]), axis=0)
                best = c[np.argmin(s, axis=0), v]
                back = L[np.clip(m[None, :] + 1 - j, 0, 15), v[None, :]]
                nl[q, g] = np.where(j == 0, best[None, :], np.where(j <= m[None, :], back, c)); nz[q, g] = Z
                y = (Z + X[:, best]) >> 1
                x[q, g][:, S * v + (u & (S - 1))] = y
                ncut[q] += int(np.count_nonzero(m < 15))
        l = nl; cut = ncut
    return {"yl": l.reshape(N, 128, TU).astype(np.float32), "yz": nz.reshape(N, 128, TU).astype(np.float32)}

@@ -1,0 +1,529 @@
+from concourse.mybir import dt, AluOpType, ActivationFunctionType
+
+N, RO, TU, BL = 8, 4, 256, 128
+HOPS = [4, 1]
+NE = 8
+A_ = AluOpType
+F_ = ActivationFunctionType
+BIG = 1.5 * 2.0 ** 35
+
+SCRATCH = {}
+
+
+def buf(name, cols, dtype, where="sbuf"):
+    SCRATCH[name] = (where, [128, cols], dtype)
+
+
+for _n in ("xs", "gg", "mm", "hb", "hh", "aa"):
+    buf(_n, 4096, "bfloat16")
+buf("l0", 256, "int32"); buf("lo0", 256, "uint16")
+buf("rel", BL * 3, "uint16"); buf("land", BL * 6, "uint16"); buf("nb", BL * 6, "uint16")
+PART = {}
+for _t in range(1, RO):
+    PART["rel%d" % _t] = ("rel", BL * (_t - 1))
+    for _b in (0, 1):
+        PART["land%d%d" % (_t, _b)] = ("land", BL * (2 * _t - 2 + _b))
+        PART["nb%d%d" % (_t, _b)] = ("nb", BL * (2 * _t - 2 + _b))
+
+
+def at(name, a=0, b=BL):
+    n, o = PART[name]
+    return n, o + a, o + b
+
+
+for _b in (0, 1):
+    for _n, _c, _d in (("lf", 128, "float32"), ("lp", 64, "float32"), ("lq", 128, "float32"), ("sk", 1024, "float32"),
+                       ("ok", 128, "bfloat16"), ("ms", 136, "bfloat16"), ("ofm", 16, "uint16"), ("zt", 128, "bfloat16"),
+                       ("rr", 128, "float32"), ("ww", 128, "float32"), ("ci", 128, "int32"), ("cc", 128, "int32"),
+                       ("ofc", 128, "uint16"), ("ks", 128, "float32"), ("kr", 128, "float32"), ("oh", 128, "bfloat16"),
+                       ("ot", 128, "bfloat16"), ("pb", 128, "float32"), ("mt", 128, "bfloat16"), ("ofi", 8, "uint16"),
+                       ("rp", 128, "int32"), ("rv", 128, "int32"), ("rest", 128, "float32"), ("out", 128, "float32"),
+                       ("zo", 128, "float32")):
+        buf(_n + str(_b), _c, _d)
+for _n, _c, _d in (("xl", 256, "bfloat16"), ("zz", 256, "bfloat16"), ("yi", 256, "int32"), ("y2", 256, "int32"),
+                   ("ofs", 16, "uint16"), ("uw", 16, "int32"), ("u15", 16, "int32"), ("uv", 16, "int32"),
+                   ("ei", 1, "int32"), ("ea", 1, "int32"), ("thr", 4, "float32"), ("nth", 4, "float32"),
+                   ("bm", 128, "float32"), ("km", 128, "float32"), ("kq", 8, "float32"), ("kd", 8, "int32"),
+                   ("csf", 16, "float32"), ("cvf", 16, "float32"),
+                   ("wi", 1, "int32"), ("ki", 1, "int32"), ("li", 4, "int32"),
+                   ("pc", 1, "int32"), ("pi", 1, "int32"), ("pg", 1, "int32"), ("row", 128, "int32"), ("r15", 128, "int32"),
+                   ("r16", 128, "int32"), ("cols", 24, "float32"), ("tq", 128, "float32"),
+                   ("bo", 128, "bfloat16"), ("qp", 128, "bfloat16"),
+                   ("mk", 136, "bfloat16"), ("idb", 128, "bfloat16"), ("nid", 128, "bfloat16"), ("idf", 128, "float32"),
+                   ("r0f", 128, "float32"), ("bom", 136, "bfloat16"), ("boi", 128, "bfloat16"), ("wb", 128, "bfloat16"),
+                   ("ind", 2048, "bfloat16"), ("wr", 2048, "bfloat16"), ("sh", 1920, "float32"), ("ex", 2048, "bfloat16"),
+                   ("ones", 2048, "bfloat16"), ("rst", 1024, "bfloat16"), ("rs2", 128, "float32"), ("kc", 128, "bfloat16"),
+                   ("irow", 128, "bfloat16"), ("cr", 16, "float32"), ("cw", 16, "float32"), ("cv", 16, "bfloat16"),
+                   ("cvs", 16, "int32"), ("cs", 16, "bfloat16"), ("g8", 8, "bfloat16"), ("koi", 8, "int32"), ("kof", 8, "uint16")):
+    buf(_n, _c, _d)
+for _n in range(8):
+    buf("q%d" % _n, 512, "float32", "psum")
+
+SEMAPHORES = ["sV", "sS", "sT", "sG", "dx", "dt", "dw", "dk", "dl", "lsem", "o00", "o01", "o10", "o11"]
+SEMAPHORES += ["a%d%d" % (_t, _b) for _t in range(1, RO) for _b in (0, 1)] + ["h%d" % _t for _t in range(1, RO)]
+
+BIG16 = 1.5 * 2.0 ** 27
+TAIL = 0
+CH = 64
+
+CYC, TEC = 0.00083, 0.000417
+
+
+def build():
+    ops = []
+
+    def add(q, cost, fn, rd, wr, n=1, late=0.0, gat=False):
+        ops.append(dict(q=q, c=cost, fn=fn, rd=rd, wr=wr, n=n, late=late, gat=gat))
+
+    def whole(*names):
+        return [(x, 0, SCRATCH[x][1][1]) for x in names]
+
+    def R(x):
+        return [y if isinstance(y, tuple) else at(y) if y in PART else whole(y)[0] for y in x]
+
+    def V(cyc, fn, rd, wr):
+        add("V", max(64, cyc) * CYC + 0.02, lambda e, T: [fn(e, T)], R(rd), R(wr))
+
+    def S(cyc, fn, rd, wr):
+        add("S", cyc * CYC + 0.065, lambda e, T: [fn(e, T)], R(rd), R(wr))
+
+    def TE(cyc, fn, rd, wr, n=1):
+        add("T", cyc * TEC + 0.03, fn, R(rd), R(wr), n)
+
+    def GP(cyc, fn, rd, wr):
+        add("G", 0.17 + cyc * CYC, lambda e, T: [fn(e, T)], R(rd), R(wr))
+
+    def ev(sem, val, buf, late):
+        add("E", 0.0, (sem, val), [], R([buf]), 0, late)
+
+    def ts(out, in0, s1, s2, *op):
+        return lambda e, T: e.tensor_scalar(out(T), in0(T), s1(T) if callable_(s1) else s1, s2(T) if callable_(s2) else s2, *op)
+
+    def callable_(x):
+        return not isinstance(x, (int, float)) and x is not None
+
+    def tt(out, a, b, op):
+        return lambda e, T: e.tensor_tensor(out(T), a(T), b(T), op)
+
+    def tc(out, a):
+        return lambda e, T: e.tensor_copy(out(T), a(T))
+
+    def P(name, a=None, b=None):
+        if name in PART:
+            name, a, b = at(name) if a is None else at(name, a, b)
+        return (lambda T: T[name][:, :]) if a is None else (lambda T: T[name][:, a:b])
+
+    def col(j):
+        return P("cols", j, j + 1)
+
+    ev("dx", 16, "xs", 6.0); ev("dt", 16, "l0", 3.0); ev("dw", 16, "wi", 2.5); ev("dk", 16, "ki", 2.5); ev("dl", 16, "li", 2.5)
+    GP(2, lambda e, T: e.iota(T.pc[:, :], [[0, 1]], 0, 1), [], ["pc"])
+    GP(256, lambda e, T: e.iota(T.row[:, :], [[1, 128]], 0, 0), [], ["row"])
+    GP(16, lambda e, T: e.iota(T.koi[:, :], [[16, 8]], 15, 0), [], ["koi"])
+    GP(32, lambda e, T: e.iota(T.cr[:, :], [[1, 16]], 0, 0, allow_small_or_imprecise_dtypes=True), [], ["cr"])
+    GP(32, lambda e, T: e.iota(T.cw[:, :], [[0, 4], [16, 4]], 0, 0, allow_small_or_imprecise_dtypes=True), [], ["cw"])
+    V(1024, lambda e, T: e.memset(T.ones[:, :], 1.0), [], ["ones"])
+    GP(4096, lambda e, T: e.affine_select(T.ex[:, :], T.ones[:, :], [[-1, 128], [0, 16]], A_.is_equal, 0.0, 0, 1), ["ones"], ["ex"])
+    V(512, lambda e, T: e.memset(T.rst[:, :], 0.0), [], ["rst"])
+    V(64, lambda e, T: e.memset(T.rst[:, 0::16], 1024.0), [], ["rst"])
+    V(128, lambda e, T: e.memset(T.rs2[:, :], 0.0), [], ["rs2"])
+    V(64, lambda e, T: e.memset(T.rs2[:, 0::16], 1048576.0), [], ["rs2"])
+    V(64, lambda e, T: e.memset(T.kc[:, :], 0.5), [], ["kc"])
+    V(64, lambda e, T: e.memset(T.kc[0:1, :], -2048.0), [], ["kc"])
+    for b in (0, 1):
+        V(64, lambda e, T, b=b: e.memset(T["sk%d" % b][:, 0:64], 0.0), [], [("sk%d" % b, 0, 64)])
+    V(1, ts(P("pi"), P("pc"), 15, None, A_.bitwise_and), ["pc"], ["pi"])
+    V(1, ts(P("pg"), P("pc"), 112, None, A_.bitwise_and), ["pc"], ["pg"])
+    V(1, tc(col(0), P("pi")), ["pi"], [("cols", 0, 1)])
+    V(1, tc(col(1), P("pg")), ["pg"], [("cols", 1, 2)])
+    V(1, ts(col(2), P("pi"), 1.0, None, A_.is_ge), ["pi"], [("cols", 2, 3)])
+    V(1, ts(col(3), P("pi"), 15.0, None, A_.is_ge), ["pi"], [("cols", 3, 4)])
+    V(1, ts(col(4), col(2), 20.75, -20.0, A_.mult, A_.add), [("cols", 2, 3)], [("cols", 4, 5)])
+    V(1, ts(col(5), P("pi"), 16.0, None, A_.mult), ["pi"], [("cols", 5, 6)])
+    V(1, ts(col(6), P("pg"), 0.0625, None, A_.mult), ["pg"], [("cols", 6, 7)])
+    V(1, tc(col(7), P("wi")), ["wi"], [("cols", 7, 8)])
+    V(1, ts(col(8), P("ki"), 8.0, 2047.5, A_.mult, A_.add), ["ki"], [("cols", 8, 9)])
+    V(1, tc(col(10), P("ki")), ["ki"], [("cols", 10, 11)])
+    V(1, ts(col(9), P("ki"), col(10), -64.0, A_.mult, A_.mult), ["ki", ("cols", 10, 11)], [("cols", 9, 10)])
+    V(1, tc(P("thr", 0, 1), P("li", 0, 1)), ["li"], [("thr", 0, 1)])
+    V(1, ts(P("nth", 0, 1), P("li", 0, 1), -1.0, 0.5, A_.mult, A_.add), ["li"], [("nth", 0, 1)])
+    V(128, ts(P("r15"), P("row"), 15, None, A_.bitwise_and), ["row"], ["r15"])
+    V(128, ts(P("r16"), P("row"), 112, None, A_.bitwise_and), ["row"], ["r16"])
+    c = lambda j: ("cols", j, j + 1)
+    V(128, ts(P("bo"), P("r16"), col(1), None, A_.is_equal), ["r16", c(1)], ["bo"])
+    V(128, ts(P("tq"), P("r15"), 1.0, None, A_.add), ["r15"], ["tq"])
+    V(256, tt(P("qp"), P("tq"), P("bo"), A_.mult), ["tq", "bo"], ["qp"])
+    for i in range(16):
+        V(64, ts(P("ind", 128 * i, 128 * i + 128), P("qp"), float(i + 1), None, A_.is_equal), ["qp"], [("ind", 128 * i, 128 * i + 128)])
+    V(128, ts(P("mk", 0, 128), P("r15"), col(0), None, A_.is_equal), ["r15", c(0)], [("mk", 0, 128)])
+    V(1, lambda e, T: e.memset(T.mk[:, 128:136], 1.0), [], [("mk", 128, 136)])
+    V(128, ts(P("bom", 0, 128), P("bo"), col(2), None, A_.mult), ["bo", c(2)], [("bom", 0, 128)])
+    V(1, tc(P("bom", 128, 129), col(3)), [c(3)], [("bom", 128, 129)])
+    V(64, ts(P("boi"), P("bo"), col(0), None, A_.mult), ["bo", c(0)], ["boi"])
+    V(64, ts(P("wb"), P("bo"), col(7), None, A_.mult), ["bo", c(7)], ["wb"])
+    V(256, tt(P("idb"), P("bo"), P("mk", 0, 128), A_.mult), ["bo", ("mk", 0, 128)], ["idb"])
+    S(128, lambda e, T: e.activation(T.nid[:, :], T.idb[:, :], F_.Copy, scale=-1.0), ["idb"], ["nid"])
+    S(128, lambda e, T: e.activation(T.idf[:, :], T.idb[:, :], F_.Copy), ["idb"], ["idf"])
+    V(128, ts(P("r0f"), P("qp"), 1.0, None, A_.is_equal), ["qp"], ["r0f"])
+    V(128, tc(P("irow"), P("r15")), ["r15"], ["irow"])
+    V(64, ts(P("cs", 0, 8), P("cr", 0, 8), col(6), None, A_.is_equal), ["cr", c(6)], [("cs", 0, 8)])
+    V(64, ts(P("cs", 8, 16), P("cr", 0, 8), col(6), 64.0, A_.is_equal, A_.mult), ["cr", c(6)], [("cs", 8, 16)])
+    V(64, ts(P("g8"), P("cr", 0, 8), col(6), 16.0, A_.is_equal, A_.mult), ["cr", c(6)], ["g8"])
+    V(64, ts(P("cv", 0, 8), P("cr", 0, 8), 256.0, col(5), A_.mult, A_.add), ["cr", c(5)], [("cv", 0, 8)])
+    V(64, ts(P("cv", 8, 16), P("cw", 0, 8), col(0), None, A_.add), ["cw", c(0)], [("cv", 8, 16)])
+    V(64, ts(P("cvs"), P("cr"), 256.0, col(5), A_.mult, A_.add), ["cr", c(5)], ["cvs"])
+    V(64, tc(P("kof"), P("koi")), ["koi"], ["kof"])
+    V(128, ts(P("bm"), P("qp"), 2.0, col(2), A_.is_ge, A_.mult), ["qp", c(2)], ["bm"])
+    for y in range(1, 16):
+        GP(256, lambda e, T, y=y: e.affine_select(T.sh[:, 128 * (y - 1):128 * y], T.bm[:, :], [[-16, 8], [1, 16]], A_.is_equal, 0.0, -(y + 1), 1), ["bm"], [("sh", 128 * (y - 1), 128 * y)])
+    S(2048, lambda e, T: e.activation(T.wr[:, :], T.ind[:, :], F_.Copy, scale=T.cols[:, 7:8]), ["ind", c(7)], ["wr"])
+    V(64, ts(P("csf", 0, 8), P("cr", 0, 8), col(6), None, A_.is_equal), ["cr", c(6)], [("csf", 0, 8)])
+    V(64, ts(P("csf", 8, 16), P("cr", 0, 8), col(6), None, A_.is_equal), ["cr", c(6)], [("csf", 8, 16)])
+    V(64, lambda e, T: e.memset(T.cvf[:, 0:8], -7.5), [], [("cvf", 0, 8)])
+    V(64, ts(P("cvf", 8, 16), P("cr", 0, 8), 256.0, col(5), A_.mult, A_.add), ["cr", c(5)], [("cvf", 8, 16)])
+
+    def mm(e, out, l, r, st, sp):
+        return e.matmul(out, l, r, st, sp)
+
+    for t in range(RO):
+        first = len(ops)
+        for b in (1 - TAIL, TAIL):
+            tag(ops, first, 1 - b)
+            first = len(ops)
+            sb = str(b)
+            QA, QB, QC, QD = "q%d" % (2 * b), "q%d" % (2 * b + 1), "q%d" % (4 + 2 * b), "q%d" % (5 + 2 * b)
+            o = 2048 * b
+            if t == 0:
+                off = lambda v0, v1, b=b: P("lo0", 128 * b + v0, 128 * b + v1)
+                V(128, tc(P("lo0", 128 * b, 128 * b + 128), P("l0", 128 * b, 128 * b + 128)), [("l0", 128 * b, 128 * b + 128)], [("lo0", 128 * b, 128 * b + 128)])
+                ob = ("lo0", 128 * b, 128 * b + 128)
+                V(128, tc(P("lf" + sb), P("l0", 128 * b, 128 * b + 128)), [("l0", 128 * b, 128 * b + 128)], ["lf" + sb])
+            else:
+                ln = "land%d%d" % (t, b)
+                ops.append(dict(q="E", c=0.0, fn=("a%d%d" % (t, b), NE), rd=[], wr=R([ln]), n=0, late=4.5 if b else 2.8, after=(t - 1, b)))
+                off = lambda v0, v1, ln=ln: P(ln, v0, v1)
+                ob = at(ln)
+                V(128, tc(P("lf" + sb), P(ln)), [ln], ["lf" + sb])
+
+            for v0 in range(0, 128, CH):
+                c0, c1 = o + 16 * v0, o + 16 * (v0 + CH)
+                gat(add, "gg", c0, c1, off(v0, v0 + CH), ob)
+                V((c1 - c0) // 2, lambda e, T, c0=c0, c1=c1: e.tensor_tensor_scan(T.mm[:, c0:c1], T.rst[:, 0:c1 - c0], T.gg[:, c0:c1], 0.0, A_.add, A_.min),
+                  ["rst", ("gg", c0, c1)], [("mm", c0, c1)])
+                held(add, c0, c1, t)
+                TE(16 * 64, lambda e, T, v0=v0, c0=c0, c1=c1, QA=QA, CH=CH: [e.matmul(T[QA][:, v0:v0 + CH], T.ind[:, 128 * i:128 * i + 128], T.hb[:, c0 + i:c1:16], i == 0, i == 15) for i in range(16)],
+                   ["ind", ("hb", c0, c1)], [(QA, v0, v0 + CH)], 16)
+            S(128, lambda e, T, sb=sb: e.activation(T["lq" + sb][:, :], T["lf" + sb][:, :], F_.Identity, bias=T.cols[:, 9:10], scale=16.0), ["lf" + sb, c(9)], ["lq" + sb])
+            S(64, lambda e, T, sb=sb, QD=QD: e.activation(T[QD][:, 0:64], T["lf" + sb][:, 0:64], F_.Copy, scale=4096.0), ["lf" + sb], [(QD, 0, 64)])
+            V(64, tt(P("lp" + sb), P("lf" + sb, 64, 128), P(QD, 0, 64), A_.add), ["lf" + sb, (QD, 0, 64)], ["lp" + sb])
+            for Q, y0, y1 in ((QC, 1, 8), (QD, 8, 16)):
+                n = y1 - y0
+                TE(n * 256, lambda e, T, Q=Q, y0=y0, y1=y1, sb=sb: [e.matmul(T[Q][:, 64 * (y - y0):64 * (y - y0) + 64], T.sh[:, 128 * (y - 1):128 * y], T["lp" + sb][:, :], True, True) for y in range(y0, y1)],
+                   ["sh", "lp" + sb], [(Q, 0, 64 * n)], n)
+                S(64 * n, lambda e, T, Q=Q, n=n, y0=y0, sb=sb: e.activation(T["sk" + sb][:, 64 * y0:64 * y0 + 64 * n], T[Q][:, 0:64 * n], F_.Copy), [(Q, 0, 64 * n)], [("sk" + sb, 64 * y0, 64 * y0 + 64 * n)])
+            V(128, ts(P("ok" + sb), P(QA, 0, 128), col(4), None, A_.is_ge), [(QA, 0, 128), c(4)], ["ok" + sb])
+            TE(129, lambda e, T, sb=sb, QA=QA: [e.matmul(T[QA][:, 128:257], T["ok" + sb][:, :], T.bom[:, 0:129], True, True)], ["ok" + sb, ("bom", 0, 129)], [(QA, 128, 257)])
+            V(129, tt(P("ms" + sb, 0, 129), P("mk", 0, 129), P(QA, 128, 257), A_.mult), ["mk", (QA, 128, 257)], [("ms" + sb, 0, 129)])
+            TE(128, lambda e, T, sb=sb, QA=QA: [e.matmul(T[QA][:, 264:280], T["ms" + sb][:, 0:128], T.cs[:, :], True, False), e.matmul(T[QA][:, 264:280], T.idb[:, :], T.cv[:, :], False, True)],
+               [("ms" + sb, 0, 129), "cs", "idb", "cv"], [(QA, 264, 280)], 2)
+            V(64, tc(P("ofm" + sb), P(QA, 264, 280)), [(QA, 264, 280)], ["ofm" + sb])
+            gat(add, "xl", 128 * b, 128 * b + 128, P("ofm" + sb, 0, 8), ("ofm" + sb, 0, 16), ("gg", o, o + 2048))
+            gat(add, "zz", 128 * b, 128 * b + 128, P("ofm" + sb, 0, 8), ("ofm" + sb, 0, 16), ("mm", o, o + 2048))
+            TE(192, lambda e, T, b=b, QB=QB: [e.matmul(T[QB][:, 0:128], T.wb[:, :], T.xl[:, 128 * b:128 * b + 128], True, False), e.matmul(T[QB][:, 0:128], T.kc[0:2, :], T.ones[0:2, 0:128], False, True)],
+               ["wb", ("xl", 128 * b, 128 * b + 128), "kc", "ones"], [(QB, 0, 128)], 2)
+            V(128, ts(P("rr" + sb), P(QB, 0, 128), BIG, BIG, A_.add, A_.subtract), [(QB, 0, 128)], ["rr" + sb])
+            V(128, tt(P("ww" + sb), P(QB, 0, 128), P("rr" + sb), A_.subtract), [(QB, 0, 128), "rr" + sb], ["ww" + sb])
+            S(128, lambda e, T, sb=sb, QB=QB: e.activation(T[QB][:, 128:256], T["ww" + sb][:, :], F_.Square, bias=T.cols[:, 8:9]), ["ww" + sb, c(8)], [(QB, 128, 256)])
+            V(128, tt(P("ci" + sb), P("lq" + sb), P(QB, 128, 256), A_.add), ["lq" + sb, (QB, 128, 256)], ["ci" + sb])
+            V(128, ts(P("cc" + sb), P("ci" + sb), 4, 4095, A_.arith_shift_right, A_.bitwise_and), ["ci" + sb], ["cc" + sb])
+            V(128, tc(P("ofc" + sb), P("cc" + sb)), ["cc" + sb], ["ofc" + sb])
+            TE(128, lambda e, T, b=b, QD=QD: [e.matmul(T[QD][:, 0:128], T.zz[:, 128 * b:128 * b + 128], T.nid[:, :], True, True)], [("zz", 128 * b, 128 * b + 128), "nid"], [(QD, 0, 128)])
+            S(128, lambda e, T, sb=sb, QD=QD: e.activation(T["zt" + sb][:, :], T[QD][:, 0:128], F_.Copy), [(QD, 0, 128)], ["zt" + sb])
+            for k in range(4):
+                Q = (QC, QD)[k % 2]
+                c0, c1 = o + 512 * k, o + 512 * k + 512
+                gat(add, "hh", c0, c1, P("ofc" + sb, 32 * k, 32 * k + 32), ("ofc" + sb, 0, 128))
+                TE(1024, lambda e, T, Q=Q, c0=c0, c1=c1, k=k, sb=sb: [e.matmul(T[Q][:, :], T["zt" + sb][:, :], T.ex[:, 512 * k:512 * k + 512], True, False), e.matmul(T[Q][:, :], T.idb[:, :], T.hh[:, c0:c1], False, True)],
+                   ["zt" + sb, "ex", "idb", ("hh", c0, c1)], [Q], 2)
+                S(512, lambda e, T, Q=Q, c0=c0, c1=c1: e.activation(T.aa[:, c0:c1], T[Q][:, :], F_.Abs), [Q], [("aa", c0, c1)])
+            V(270, lambda e, T, sb=sb: e.tensor_copy(T["rp" + sb][:, :], T["sk" + sb][:, :].indirect(T["ofm" + sb][:, 8:16])), ["sk" + sb, ("ofm" + sb, 0, 16)], ["rp" + sb])
+            V(64, ts(P("rv" + sb, 0, 64), P("rp" + sb, 0, 64), 12, None, A_.arith_shift_right), ["rp" + sb], [("rv" + sb, 0, 64)])
+            V(64, ts(P("rv" + sb, 64, 128), P("rp" + sb, 64, 128), 4095, None, A_.bitwise_and), ["rp" + sb], [("rv" + sb, 64, 128)])
+            TE(256, lambda e, T, sb=sb, QA=QA: [e.matmul(T[QA][:, 280:408], T.nid[:, :], T["ok" + sb][:, :], True, False), e.matmul(T[QA][:, 280:408], T.ones[0:1, 0:128], T.ones[0:1, 0:128], False, True)],
+               ["nid", "ok" + sb, "ones"], [(QA, 280, 408)], 2)
+            V(128, tt(P(QA, 0, 128), P("cc" + sb), P(QA, 280, 408), A_.mult), ["cc" + sb, (QA, 280, 408)], [(QA, 0, 128)])
+            V(128, tt(P("rest" + sb), P("rv" + sb), P(QA, 0, 128), A_.add), ["rv" + sb, (QA, 0, 128)], ["rest" + sb])
+            TE(16 * 64 + 128, lambda e, T, o=o, QB=QB: [e.matmul(T[QB][:, 384:512], T.ones[0:1, 0:128], T.irow[0:1, :], True, False)] +
+               [e.matmul(T[QB][:, 384 + i:512:16], T.aa[:, o + i:o + 2048:16], T.g8[:, :], False, i == 15) for i in range(16)],
+               ["ones", "irow", ("aa", o, o + 2048), "g8"], [(QB, 384, 512)], 17)
+            V(128, lambda e, T, sb=sb, QB=QB: e.tensor_tensor_scan(T["ks" + sb][:, :], T.rs2[:, :], T[QB][:, 384:512], 0.0, A_.add, A_.min), ["rs2", (QB, 384, 512)], ["ks" + sb])
+            V(270, lambda e, T, sb=sb: e.tensor_copy(T["kr" + sb][:, :], T["ks" + sb][:, :].indirect(T.kof[:, :])), ["ks" + sb, "kof"], ["kr" + sb])
+            V(128, tt(P("oh" + sb), P("kr" + sb), P(QB, 384, 512), A_.is_equal), ["kr" + sb, (QB, 384, 512)], ["oh" + sb])
+            TE(128, lambda e, T, sb=sb, QA=QA: [e.matmul(T[QA][:, 0:128], T["oh" + sb][:, :], T.idb[:, :], True, True)], ["oh" + sb, "idb"], [(QA, 0, 128)])
+            V(128, tt(P("pb" + sb), P("cc" + sb), P(QA, 0, 128), A_.mult), ["cc" + sb, (QA, 0, 128)], ["pb" + sb])
+            TE(512, lambda e, T, sb=sb, QD=QD: [e.matmul(T[QD][:, 0:128], T.idf[:, :], T["rest" + sb][:, :], True, False)], ["idf", "rest" + sb], [(QD, 0, 128)])
+            TE(512, lambda e, T, sb=sb, QD=QD: [e.matmul(T[QD][:, 0:128], T.r0f[:, :], T["pb" + sb][:, :], False, True)], ["r0f", "pb" + sb], [(QD, 0, 128)])
+            if t < RO - 1:
+                nb = "nb%d%d" % (t + 1, b)
+                V(128, tc(P(nb), P(QD, 0, 128)), [(QD, 0, 128)], [nb])
+                ops.append(dict(q="G", c=1.0, fn=None, rd=R([nb]), wr=[], n=0, late=0.0, send=(t, b, nb)))
+                if b == TAIL:
+                    V(256, tt(P("km"), P("kr" + sb), P("mk", 0, 128), A_.mult), ["kr" + sb, ("mk", 0, 128)], ["km"])
+                    TE(512, lambda e, T, QA=QA: [e.matmul(T[QA][:, 264:280], T.idf[:, :], T.cvf[:, :], True, False), e.matmul(T[QA][:, 264:280], T.km[:, :], T.csf[:, :], False, True)],
+                       ["km", "csf", "idf", "cvf"], [(QA, 264, 280)], 2)
+                    V(8, ts(P("kq"), P(QA, 264, 272), BIG16, BIG16, A_.add, A_.subtract), [(QA, 264, 280)], ["kq"])
+                    V(8, tt(P("kd"), P(QA, 272, 280), P("kq"), A_.subtract), [(QA, 264, 280), "kq"], ["kd"])
+                    V(8, tc(P("ofi" + sb), P("kd")), ["kd"], ["ofi" + sb])
+                else:
+                  S(128, lambda e, T, sb=sb, QA=QA: e.activation(T["ot" + sb][:, :], T[QA][:, 0:128], F_.Copy), [(QA, 0, 128)], ["ot" + sb])
+                  TE(128, lambda e, T, sb=sb, QA=QA: [e.matmul(T[QA][:, 128:256], T["ot" + sb][:, :], T.boi[:, :], True, True)], ["ot" + sb, "boi"], [(QA, 128, 256)])
+                  V(128, tt(P("mt" + sb), P("mk", 0, 128), P(QA, 128, 256), A_.mult), ["mk", (QA, 128, 256)], ["mt" + sb])
+                  TE(128, lambda e, T, sb=sb, QA=QA: [e.matmul(T[QA][:, 264:272], T["mt" + sb][:, :], T.cs[:, 0:8], True, False), e.matmul(T[QA][:, 264:272], T.idb[:, :], T.cv[:, 0:8], False, True)],
+                   ["mt" + sb, "cs", "idb", "cv"], [(QA, 264, 272)], 2)
+                  V(64, tc(P("ofi" + sb), P(QA, 264, 272)), [(QA, 264, 272)], ["ofi" + sb])
+                h0, h1 = 128 * b, 128 * b + 128
+                V(270, lambda e, T, sb=sb, o=o, h0=h0, h1=h1: e.tensor_tensor(T.yi[:, h0:h1], T.hh[:, o:o + 2048].indirect(T["ofi" + sb][:, :]), T.zz[:, h0:h1], A_.add),
+                  [("hh", o, o + 2048), "ofi" + sb, ("zz", h0, h1)], [("yi", h0, h1)])
+                V(128, ts(P("y2", h0, h1), P("yi", h0, h1), 1, None, A_.arith_shift_right), [("yi", h0, h1)], [("y2", h0, h1)])
+            else:
+                h0, h1 = 128 * b, 128 * b + 128
+                V(128, tc(P("out" + sb), P(QD, 0, 128)), [(QD, 0, 128)], ["out" + sb])
+                S(128, lambda e, T, sb=sb, h0=h0, h1=h1: e.activation(T["zo" + sb][:, :], T.zz[:, h0:h1], F_.Copy), [("zz", h0, h1)], ["zo" + sb])
+                ops.append(dict(q="Y", c=0.1, fn=("yz", h0, h1, "zo" + sb, "o0" + sb), rd=R(["zo" + sb]), wr=[], n=0, late=2.0))
+                ops.append(dict(q="Y", c=0.1, fn=("yl", h0, h1, "out" + sb, "o1" + sb), rd=R(["out" + sb]), wr=[], n=0, late=2.0))
+        tag(ops, first, TAIL)
+        if t < RO - 1:
+            TE(128, lambda e, T: [e.matmul(T.q0[:, 408:409], T.ones[:, 0:128], T.ms1[:, 128:129], True, False), e.matmul(T.q0[:, 408:409], T.ones[:, 0:128], T.ms0[:, 128:129], False, True)],
+               ["ones", ("ms0", 128, 129), ("ms1", 128, 129)], [("q0", 408, 409)], 2)
+            V(1, ts(P("ei"), P("q0", 408, 409), -1.0, 2048.0, A_.mult, A_.add), [("q0", 408, 409)], ["ei"])
+            V(1, ts(P("ea"), P("ei"), 7, None, A_.bitwise_and), ["ei"], ["ea"])
+            V(1, tt(P("thr", t + 1, t + 2), P("li", t + 1, t + 2), P("ea"), A_.add), ["li", "ea"], [("thr", t + 1, t + 2)])
+            V(1, ts(P("nth", t + 1, t + 2), P("thr", t + 1, t + 2), -1.0, 0.5, A_.mult, A_.add), [("thr", t + 1, t + 2)], [("nth", t + 1, t + 2)])
+            TE(16 * 64, lambda e, T: [e.matmul(T.q2[:, 416:432], T.wr[:, 128 * r:128 * r + 128], T.xl[:, r::16], r == 0, r == 15) for r in range(16)], ["wr", "xl"], [("q2", 416, 432)], 16)
+            V(64, tc(P("uw"), P("q2", 416, 432)), [("q2", 416, 432)], ["uw"])
+            V(64, ts(P("u15"), P("uw"), 15, None, A_.bitwise_and), ["uw"], ["u15"])
+            V(64, tt(P("uv"), P("u15"), P("cvs"), A_.add), ["u15", "cvs"], ["uv"])
+            V(64, tc(P("ofs"), P("uv")), ["uv"], ["ofs"])
+            for b in (1, 0):
+                V(540, lambda e, T, b=b: e.tensor_copy(T.xs[:, :].indirect(T.ofs[:, 8 * b:8 * b + 8]), T.y2[:, 128 * b:128 * b + 128]),
+                  [("y2", 128 * b, 128 * b + 128), "ofs"], ["xs"])
+    return ops
+
+
+def tag(ops, first, b):
+    for op in ops[first:]:
+        op["b"] = b
+
+
+def gat(add, dst, c0, c1, off, ob, win=("xs", 0, 4096), q="VS"):
+    def fn(e, T, scalar):
+        src = T[win[0]][:, win[1]:win[2]].indirect(off(T))
+        return [e.activation(T[dst][:, c0:c1], src, F_.Copy) if scalar else e.tensor_copy(T[dst][:, c0:c1], src)]
+    n = c1 - c0
+    add(q, {"V": 0.06 + n * 1.56 * CYC, "S": 0.075 + n * 1.56 * CYC}, fn, [win, ob], [(dst, c0, c1)], 1, 0.0, True)
+
+
+def held(add, c0, c1, t):
+    def fn(e, T, scalar):
+        if scalar:
+            return [e.activation(T.hb[:, c0:c1], T.mm[:, c0:c1], F_.Sign, bias=T.nth[:, t:t + 1])]
+        return [e.tensor_scalar(T.hb[:, c0:c1], T.mm[:, c0:c1], T.thr[:, t:t + 1], 0.5, A_.is_ge, A_.subtract)]
+    n = c1 - c0
+    add("VS", {"V": 0.02 + n * 0.5 * CYC, "S": 0.065 + n * CYC}, fn, [("mm", c0, c1), ("thr", t, t + 1), ("nth", t, t + 1)], [("hb", c0, c1)], 1, 0.0, True)
+
+
+def link(ops):
+    hist = {}
+    for k, op in enumerate(ops):
+        deps, order = set(), set()
+        acc = [(r, False) for r in op["rd"]] + [(w, True) for w in op["wr"]]
+        for (bn, a, z), wr in acc:
+            ps = SCRATCH[bn][0] == "psum"
+            for (a2, z2, k2, w2) in hist.get(bn, []):
+                if k2 == k:
+                    continue
+                over = a < z2 and a2 < z
+                if ps:
+                    same = op["q"] == ops[k2]["q"]
+                    if not same:
+                        deps.add(k2)
+                    elif over and w2 and op["q"] != "T":
+                        deps.add(k2)
+                    else:
+                        order.add(k2)
+                elif over and (wr or w2):
+                    if w2:
+                        deps.add(k2)
+                    elif op["q"] == ops[k2]["q"] and len(op["q"]) == 1:
+                        order.add(k2)
+                    else:
+                        deps.add(k2)
+        for (bn, a, z), wr in acc:
+            h = hist.setdefault(bn, [])
+            if wr and SCRATCH[bn][0] != "psum":
+                h[:] = [x for x in h if not (a <= x[0] and x[1] <= z)]
+            if SCRATCH[bn][0] == "psum":
+                h[:] = [x for x in h if not (x[2] in deps and (ops[x[2]]["q"] != op["q"] or (a <= x[0] and x[1] <= z)))]
+            h.append((a, z, k, wr))
+        if op.get("after") is not None:
+            for k2 in range(k):
+                if ops[k2].get("send", (None,))[:2] == op["after"]:
+                    order.add(k2)
+        op["deps"], op["order"] = deps, order - deps
+
+
+LAT = 0.17
+
+
+def schedule(ops, bias=0.0, jit=None):
+    n = len(ops)
+    succ = [[] for _ in range(n)]
+    left = [0] * n
+    cost = [op["c"] if isinstance(op["c"], dict) else {q: op["c"] for q in op["q"]} for op in ops]
+    for k, op in enumerate(ops):
+        for d in op["deps"] | op["order"]:
+            succ[d].append(k)
+            left[k] += 1
+    prio = [0.0] * n
+    for k in range(n - 1, -1, -1):
+        op = ops[k]
+        prio[k] = min(cost[k].values()) + op["late"] + LAT + max([prio[s] for s in succ[k]], default=0.0)
+    prio = [prio[k] + (bias if ops[k].get("b", TAIL) != TAIL else 0.0) + (jit[k] if jit is not None else 0.0) for k in range(n)]
+    free = {"V": 0.0, "S": 0.0, "T": 0.0, "G": 0.0, "Y": 0.0, "E": 0.0}
+    end, est = [None] * n, [0.0] * n
+    ready = [k for k in range(n) if left[k] == 0]
+    seq = []
+    while ready:
+        cands = []
+        for k in ready:
+            f, s, q = min((max(est[k], free[q]) + cost[k][q], max(est[k], free[q]), q) for q in ops[k]["q"])
+            cands.append((s, -prio[k], k, q))
+        first = min(cands)[0]
+        s, p, k, q = min((x for x in cands if x[0] <= first + SLACK), key=lambda x: (x[1], x[0], x[3]))
+        op = ops[k]
+        ready.remove(k)
+        op["at"], op["on"], op["cost"] = s, q, cost[k][q]
+        end[k] = s + cost[k][q] + op["late"]
+        if q != "E":
+            free[q] = s + cost[k][q]
+        seq.append(k)
+        for x in succ[k]:
+            left[x] -= 1
+            est[x] = max(est[x], end[k] + (LAT if k in ops[x]["deps"] else 0.0))
+            if left[x] == 0:
+                ready.append(x)
+    return seq, max(end)
+
+
+SLACK = 0.0
+PLAN = {}
+ABC = "0123456789abcdefghijklmnopqrstuvwxyzABCDEFGHIJKLMNOPQRSTUVWXYZ"
+SHIFT = "Hn5HSB0sWoYXui7RA78nABE8EBZzIOZKC14QtTAQZZaTN8ozoDTEzE05yVeOQZTZZTTDOTTMLTTHlTihqMt32TxTFszH3qLsQnMCTxTbAC1AAFnSIh7T43eCeAEDRKyLTxPZVryJAGukDAHffVZZLQcXxUWtpyink8jZVuC9PQZdHZZYodZLCzvutVWZmoQVsHZBZZcsZmjUkRZdUttAmPX5xZAZPi05ZC01Q3YEd19aQtdyB7qdlI8YjKVUUbxYZfYwN3u6TRLDsNYMG4uZV0fVVM0xg0vEdcJeubm2Goyb0M3bst0DjWRnRMOCj0KnfOqXV10gdDjq0yiulFSPO2SQKX5ZOZnOPQCbXOlanw5o5fpv580Sa5u5g7f1v0yRKScQDoQFtpIZJrxANUysEuTcwZUZkQZYJiMzqZZWObdDJzmspg66EvM7moZ5NwWF7HZfCr6kaZXeBOjh0QpSoyBvmOq0Emh85KXNZeZUaLg66d6l6w6666n60000KdyR16081R6K8c03e0WOiyooMCBxS0D7MpMAQTMFK4evm4ZIFZLZP0JE1p600jPPPczs03d9C0yhJJZobdjNaHo2hP9KvBFDkZJiZbTZTuLBOQWSTuYR40jcBjzkdcKZOkk7djSt00O7pBt8hXyHWUWFRdWzZ"
+PLACE = "**VV**SVVSS***VV*SSS*VSV*VS*SVSSS*VVVSS*VVS**VVSVV**SVSSSVS**S**VSV*SV*SV**V*VV*"
+
+
+def plan():
+    if not PLAN:
+        ops = build()
+        link(ops)
+        both = [op for op in ops if len(op["q"]) > 1]
+        if len(SHIFT) == len(ops) and len(PLACE) == len(both):
+            for op, p in zip(both, PLACE):
+                op["q"] = op["q"] if p == "*" else p
+            seq, total = schedule(ops, 0.0, [(ABC.index(x) - 31) * 0.12 for x in SHIFT])
+        else:
+            seq, total = schedule(ops, 8.0)
+        PLAN["ops"], PLAN["seq"], PLAN["total"] = ops, seq, total
+    return PLAN["ops"], PLAN["seq"]
+
+
+def bits(topo, src, dst):
+    return sum(1 << e for e in topo.engines(src, dst)[:NE])
+
+
+def helper(topo, core, dst):
+    for c in topo.cores_of(core):
+        if c != core and topo.die(c) == topo.die(core) and topo.may_write(c, dst):
+            return c
+    return None
+
+
+def send(g, T, topo, core, dst, out, src, rsem):
+    rid, pid = topo.addr(dst, core)
+    (ob, o0, o1), (ib, i0, i1) = at(out), at(src)
+    g.remote_dma(out_ap=T[ob][:, o0:o1], in_ap=T[ib][:, i0:i1], remote_sem=T.sem[rsem], local_sem=T.sem["lsem"], pid=pid, routing_id=rid, dma_engine_mask=bits(topo, core, dst))
+
+
+def rank_program(g, core, T, topo):
+    rank = T.rank_of(core)
+    if rank is None:
+        for r, c in enumerate(T.cores):
+            dst = T.cores[(r + HOPS[1]) % N]
+            if not topo.may_write(c, dst) and helper(topo, c, dst) == core:
+                for t in range(1, RO):
+                    g.wait_ge(T.sem["h%d" % t], NE)
+                    send(g, T, topo, core, dst, "land%d1" % t, "rel%d" % t, "a%d1" % t)
+                g.wait_ge(T.sem["lsem"], NE * (RO - 1))
+        return
+    ops, seq = plan()
+    eng = {"V": g.vector, "S": g.scalar, "T": g.tensor, "G": g, "Y": g.sync}
+    semn = {"V": "sV", "S": "sS", "T": "sT", "G": "sG"}
+    g.sync.dma_start(T.xs[:, :], T.field[:, :]).then_inc(T.sem["dx"], 16)
+    g.scalar.dma_start(T.l0[:, :], T.tube[:, :]).then_inc(T.sem["dt"], 16)
+    g.scalar.dma_start(T.wi[:, :], T.wt[:, :]).then_inc(T.sem["dw"], 16)
+    g.scalar.dma_start(T.ki[:, :], T.kn[:, :]).then_inc(T.sem["dk"], 16)
+    g.scalar.dma_start(T.li[:, :], T.lim[:, :]).then_inc(T.sem["dl"], 16)
+    count = {q: 0 for q in "VSTG"}
+    known = {q: {} for q in "VSTGY"}
+    done, snap = {}, {}
+    sends = 0
+    outs = []
+    for k in seq:
+        op = ops[k]
+        q = op["on"]
+        if q == "E":
+            done[k] = op["fn"]
+            snap[k] = {}
+            continue
+        e = eng[q]
+        need = {}
+        for d in sorted(op["deps"]):
+            if d in done:
+                s, v = done[d]
+                if known[q].get(s, 0) < v and need.get(s, (0, 0))[0] < v:
+                    need[s] = (v, d)
+        for s in sorted(need):
+            v, d = need[s]
+            if any(snap[d2].get(s, 0) >= v for s2, (v2, d2) in need.items() if s2 != s):
+                continue
+            e.wait_ge(T.sem[s], v)
+        for s, (v, d) in need.items():
+            kn_ = known[q]
+            kn_[s] = max(kn_.get(s, 0), v)
+            for s2, v2 in snap[d].items():
+                kn_[s2] = max(kn_.get(s2, 0), v2)
+        snap[k] = dict(known[q])
+        if op.get("send"):
+            t, b, nb = op["send"]
+            dst = T.cores[(rank + HOPS[b]) % N]
+            if topo.may_write(core, dst):
+                send(g, T, topo, core, dst, "land%d%d" % (t + 1, b), nb, "a%d%d" % (t + 1, b))
+            else:
+                send(g, T, topo, core, helper(topo, core, dst), "rel%d" % (t + 1), nb, "h%d" % (t + 1))
+            sends += 1
+        elif q == "Y":
+            o, h0, h1, src, sm = op["fn"]
+            e.dma_start(T[o][:, h0:h1], T[src][:, :]).then_inc(T.sem[sm], 16)
+            outs.append(sm)
+        else:
+            ins = op["fn"](e, T, q == "S") if op.get("gat") else op["fn"](e, T)
+            for x in ins:
+                x.then_inc(T.sem[semn[q]], 1)
+            count[q] += len(ins)
+            done[k] = (semn[q], count[q])
+    for sm in outs:
+        g.sync.wait_ge(T.sem[sm], 16)
+    for q in "VSTG":
+        if count[q]:
+            g.sync.wait_ge(T.sem[semn[q]], count[q])
+    g.wait_ge(T.sem["lsem"], NE * sends)

@@ -2,20 +2,21 @@ from concourse.mybir import dt, AluOpType, ActivationFunctionType
 
 N, RO, TU, BL = 8, 4, 256, 128
 HOPS = [4, 1]
-NE = 8
 A_ = AluOpType
 F_ = ActivationFunctionType
-BIG = 1.5 * 2.0 ** 35
+OPT = dict(RV=1, TAIL=0, C1=(32, 64))
+COST = dict(f=1.1, gat=1.56, sca=4.0, lat=0.22, vfix=0.04, pe=0.000417, near=2.3, far=3.8, issue=1.0, dma=2.5, load=6.0)
 
 SCRATCH = {}
 
 
 def buf(name, cols, dtype, where="sbuf"):
-    SCRATCH[name] = (where, [128, cols], dtype)
+    SCRATCH[name] = (where, [128] + (cols if isinstance(cols, list) else [cols]), dtype)
 
 
-for _n in ("xs", "gg", "mm", "hb", "hh", "aa"):
+for _n in ("xs", "gg", "mm", "hb", "hh"):
     buf(_n, 4096, "bfloat16")
+buf("aa", [16, 16, 16], "bfloat16")
 buf("l0", 256, "int32"); buf("lo0", 256, "uint16")
 buf("rel", BL * 3, "uint16"); buf("land", BL * 6, "uint16"); buf("nb", BL * 6, "uint16")
 PART = {}
@@ -32,75 +33,80 @@ def at(name, a=0, b=BL):
 
 
 for _b in (0, 1):
-    for _n, _c, _d in (("lf", 128, "float32"), ("lp", 64, "float32"), ("lq", 128, "float32"), ("sk", 1024, "float32"),
-                       ("ok", 128, "bfloat16"), ("ms", 136, "bfloat16"), ("ofm", 16, "uint16"), ("zt", 128, "bfloat16"),
-                       ("rr", 128, "float32"), ("ww", 128, "float32"), ("ci", 128, "int32"), ("cc", 128, "int32"),
-                       ("ofc", 128, "uint16"), ("ks", 128, "float32"), ("kr", 128, "float32"), ("oh", 128, "bfloat16"),
-                       ("ot", 128, "bfloat16"), ("pb", 128, "float32"), ("mt", 128, "bfloat16"), ("ofi", 8, "uint16"),
-                       ("rp", 128, "int32"), ("rv", 128, "int32"), ("rest", 128, "float32"), ("out", 128, "float32"),
-                       ("zo", 128, "float32")):
+    for _n, _c, _d in (("lq", 128, "float32"), ("sk", 2048, "float32"), ("ok", 512, "bfloat16"), ("si", 128, "int32"),
+                       ("uu", 256, "int32"), ("ofm", 24, "uint16"), ("zt", 128, "bfloat16"), ("zz", 128, "float32"),
+                       ("ci", 128, "int32"), ("cc", 128, "int32"), ("ofc", 128, "uint16"), ("ofi", 8, "uint16"),
+                       ("rv", 128, "float32"), ("cm", 128, "float32"), ("out", 128, "float32"), ("zo", 128, "float32"),
+                       ("yi", 128, "int32"), ("kw", 128, "float32"), ("ka", 8, "int32"), ("kb", 8, "int32"),
+                       ("kc", 8, "int32"), ("kd", 8, "int32"), ("ofl", 8, "uint16"), ("cw", 2048, "int32")):
         buf(_n + str(_b), _c, _d)
-for _n, _c, _d in (("xl", 256, "bfloat16"), ("zz", 256, "bfloat16"), ("yi", 256, "int32"), ("y2", 256, "int32"),
-                   ("ofs", 16, "uint16"), ("uw", 16, "int32"), ("u15", 16, "int32"), ("uv", 16, "int32"),
-                   ("ei", 1, "int32"), ("ea", 1, "int32"), ("thr", 4, "float32"), ("nth", 4, "float32"),
-                   ("bm", 128, "float32"), ("km", 128, "float32"), ("kq", 8, "float32"), ("kd", 8, "int32"),
-                   ("csf", 16, "float32"), ("cvf", 16, "float32"),
+for _n, _c, _d in (("cn", 1, "bfloat16"), ("ei", 1, "int32"), ("ea", 1, "int32"), ("thr", 4, "float32"), ("nth", 4, "float32"),
                    ("wi", 1, "int32"), ("ki", 1, "int32"), ("li", 4, "int32"),
-                   ("pc", 1, "int32"), ("pi", 1, "int32"), ("pg", 1, "int32"), ("row", 128, "int32"), ("r15", 128, "int32"),
-                   ("r16", 128, "int32"), ("cols", 24, "float32"), ("tq", 128, "float32"),
-                   ("bo", 128, "bfloat16"), ("qp", 128, "bfloat16"),
-                   ("mk", 136, "bfloat16"), ("idb", 128, "bfloat16"), ("nid", 128, "bfloat16"), ("idf", 128, "float32"),
-                   ("r0f", 128, "float32"), ("bom", 136, "bfloat16"), ("boi", 128, "bfloat16"), ("wb", 128, "bfloat16"),
-                   ("ind", 2048, "bfloat16"), ("wr", 2048, "bfloat16"), ("sh", 1920, "float32"), ("ex", 2048, "bfloat16"),
-                   ("ones", 2048, "bfloat16"), ("rst", 1024, "bfloat16"), ("rs2", 128, "float32"), ("kc", 128, "bfloat16"),
-                   ("irow", 128, "bfloat16"), ("cr", 16, "float32"), ("cw", 16, "float32"), ("cv", 16, "bfloat16"),
-                   ("cvs", 16, "int32"), ("cs", 16, "bfloat16"), ("g8", 8, "bfloat16"), ("koi", 8, "int32"), ("kof", 8, "uint16")):
+                   ("pc", 1, "int32"), ("pi", 1, "int32"), ("cols", 16, "float32"), ("gs", 8, "float32"), ("gw", 8, "float32"),
+                   ("bo", 128, "bfloat16"), ("idb", 128, "bfloat16"), ("nid", 128, "bfloat16"),
+                   ("nif", 128, "float32"), ("dm", 128, "bfloat16"), ("up", 128, "bfloat16"),
+                   ("ind", 2048, "bfloat16"), ("wr", 2048, "bfloat16"), ("sh", 512, "float32"), ("ex", 2048, "bfloat16"),
+                   ("ones", 2048, "bfloat16"), ("rst", 1024, "bfloat16"), ("rs2", 128, "float32"),
+                   ("cr", 16, "float32"), ("cv", 48, "bfloat16"), ("s15", 1, "bfloat16"),
+                   ("krow", 128, "bfloat16"), ("bm", 128, "float32")):
     buf(_n, _c, _d)
 for _n in range(8):
     buf("q%d" % _n, 512, "float32", "psum")
 
-SEMAPHORES = ["sV", "sS", "sT", "sG", "dx", "dt", "dw", "dk", "dl", "lsem", "o00", "o01", "o10", "o11"]
+SEMAPHORES = ["sV", "sS", "sT", "sG", "dx", "dt", "dw", "dk", "dl", "lsem", "o00", "o01", "o10", "o11", "r00", "r01", "r10", "r11", "w0", "w1"]
 SEMAPHORES += ["a%d%d" % (_t, _b) for _t in range(1, RO) for _b in (0, 1)] + ["h%d" % _t for _t in range(1, RO)]
 
-BIG16 = 1.5 * 2.0 ** 27
-TAIL = 0
-CH = 64
 
-CYC, TEC = 0.00083, 0.000417
+def width(name):
+    n = 1
+    for x in SCRATCH[name][1][1:]:
+        n *= x
+    return n
 
 
 def build():
     ops = []
-
-    def add(q, cost, fn, rd, wr, n=1, late=0.0, gat=False):
-        ops.append(dict(q=q, c=cost, fn=fn, rd=rd, wr=wr, n=n, late=late, gat=gat))
-
-    def whole(*names):
-        return [(x, 0, SCRATCH[x][1][1]) for x in names]
+    now = {"t": -1, "b": ""}
+    TAIL, RV = OPT["TAIL"], OPT["RV"]
 
     def R(x):
-        return [y if isinstance(y, tuple) else at(y) if y in PART else whole(y)[0] for y in x]
+        return [y if isinstance(y, tuple) else at(y) if y in PART else (y, 0, width(y)) for y in x]
 
-    def V(cyc, fn, rd, wr):
-        add("V", max(64, cyc) * CYC + 0.02, lambda e, T: [fn(e, T)], R(rd), R(wr))
+    def add(name, q, cost, fn, rd, wr, **more):
+        ops.append(dict(name=name + now["b"], t=now["t"], q=q, c=cost, fn=fn, rd=R(rd), wr=R(wr), **more))
 
-    def S(cyc, fn, rd, wr):
-        add("S", cyc * CYC + 0.065, lambda e, T: [fn(e, T)], R(rd), R(wr))
+    def V(name, cyc, fn, rd, wr):
+        add(name, "V", {"V": ("v", cyc)}, lambda e, T: [fn(e, T)], rd, wr)
 
-    def TE(cyc, fn, rd, wr, n=1):
-        add("T", cyc * TEC + 0.03, fn, R(rd), R(wr), n)
+    def VG(name, n, fn, rd, wr, kind="gv"):
+        add(name, "V", {"V": (kind, n)}, lambda e, T: [fn(e, T)], rd, wr)
+
+    def S(name, cyc, fn, rd, wr):
+        add(name, "S", {"S": ("s", cyc)}, lambda e, T: [fn(e, T)], rd, wr)
+
+    def VS(name, cv, cs, fv, fs, rd, wr, kinds="vs"):
+        add(name, "VS", {"V": (kinds[0], cv), "S": (kinds[1], cs)}, lambda e, T, scalar: [(fs if scalar else fv)(e, T)], rd, wr, both=True)
+
+    def TE(name, cyc, fn, rd, wr):
+        add(name, "T", {"T": ("t", cyc)}, fn, rd, wr)
 
     def GP(cyc, fn, rd, wr):
-        add("G", 0.17 + cyc * CYC, lambda e, T: [fn(e, T)], R(rd), R(wr))
+        add("c", "G", {"G": ("g", cyc)}, lambda e, T: [fn(e, T)], rd, wr)
 
-    def ev(sem, val, buf, late):
-        add("E", 0.0, (sem, val), [], R([buf]), 0, late)
+    def C(cyc, fn, rd, wr):
+        V("c", cyc, fn, rd, wr)
+
+    def ev(sem, val, b, late, after=None):
+        add("ev", "E", {"E": ("0", 0)}, (sem, val), [], [b], late=late, after=after)
+
+    def num(x):
+        return isinstance(x, (int, float)) or x is None
+
+    def val(x, T):
+        return x if num(x) else x(T)
 
     def ts(out, in0, s1, s2, *op):
-        return lambda e, T: e.tensor_scalar(out(T), in0(T), s1(T) if callable_(s1) else s1, s2(T) if callable_(s2) else s2, *op)
-
-    def callable_(x):
-        return not isinstance(x, (int, float)) and x is not None
+        return lambda e, T: e.tensor_scalar(out(T), in0(T), val(s1, T), val(s2, T), *op)
 
     def tt(out, a, b, op):
         return lambda e, T: e.tensor_tensor(out(T), a(T), b(T), op)
@@ -108,228 +114,218 @@ def build():
     def tc(out, a):
         return lambda e, T: e.tensor_copy(out(T), a(T))
 
-    def P(name, a=None, b=None):
+    def act(out, a, func, bias=0.0, scale=1.0):
+        return lambda e, T: e.activation(out(T), a(T), func, bias=val(bias, T), scale=val(scale, T))
+
+    def scan(out, d0, d1):
+        return lambda e, T: e.tensor_tensor_scan(out(T), d0(T), d1(T), 0.0, A_.add, A_.min)
+
+    def P(name, a=None, b=None, step=None):
         if name in PART:
             name, a, b = at(name) if a is None else at(name, a, b)
-        return (lambda T: T[name][:, :]) if a is None else (lambda T: T[name][:, a:b])
+        return (lambda T: T[name][:, :]) if a is None else (lambda T: T[name][:, a:b:step]) if step else (lambda T: T[name][:, a:b])
+
+    def by(win, off):
+        return lambda T: P(*win)(T).indirect(P(*off)(T))
+
+    def gat(name, dst, win, off, scale=1.0, bias=0.0):
+        n = dst[2] - dst[1]
+        fv = tc(P(*dst), by(win, off)) if scale == 1.0 else ts(P(*dst), by(win, off), scale, bias, A_.mult, A_.add)
+        VS(name, n, n, fv, act(P(*dst), by(win, off), F_.Identity if bias else F_.Copy, bias, scale), [win, off], [dst], ("gv", "gs"))
 
     def col(j):
         return P("cols", j, j + 1)
 
-    ev("dx", 16, "xs", 6.0); ev("dt", 16, "l0", 3.0); ev("dw", 16, "wi", 2.5); ev("dk", 16, "ki", 2.5); ev("dl", 16, "li", 2.5)
-    GP(2, lambda e, T: e.iota(T.pc[:, :], [[0, 1]], 0, 1), [], ["pc"])
-    GP(256, lambda e, T: e.iota(T.row[:, :], [[1, 128]], 0, 0), [], ["row"])
-    GP(16, lambda e, T: e.iota(T.koi[:, :], [[16, 8]], 15, 0), [], ["koi"])
-    GP(32, lambda e, T: e.iota(T.cr[:, :], [[1, 16]], 0, 0, allow_small_or_imprecise_dtypes=True), [], ["cr"])
-    GP(32, lambda e, T: e.iota(T.cw[:, :], [[0, 4], [16, 4]], 0, 0, allow_small_or_imprecise_dtypes=True), [], ["cw"])
-    V(1024, lambda e, T: e.memset(T.ones[:, :], 1.0), [], ["ones"])
-    GP(4096, lambda e, T: e.affine_select(T.ex[:, :], T.ones[:, :], [[-1, 128], [0, 16]], A_.is_equal, 0.0, 0, 1), ["ones"], ["ex"])
-    V(512, lambda e, T: e.memset(T.rst[:, :], 0.0), [], ["rst"])
-    V(64, lambda e, T: e.memset(T.rst[:, 0::16], 1024.0), [], ["rst"])
-    V(128, lambda e, T: e.memset(T.rs2[:, :], 0.0), [], ["rs2"])
-    V(64, lambda e, T: e.memset(T.rs2[:, 0::16], 1048576.0), [], ["rs2"])
-    V(64, lambda e, T: e.memset(T.kc[:, :], 0.5), [], ["kc"])
-    V(64, lambda e, T: e.memset(T.kc[0:1, :], -2048.0), [], ["kc"])
-    for b in (0, 1):
-        V(64, lambda e, T, b=b: e.memset(T["sk%d" % b][:, 0:64], 0.0), [], [("sk%d" % b, 0, 64)])
-    V(1, ts(P("pi"), P("pc"), 15, None, A_.bitwise_and), ["pc"], ["pi"])
-    V(1, ts(P("pg"), P("pc"), 112, None, A_.bitwise_and), ["pc"], ["pg"])
-    V(1, tc(col(0), P("pi")), ["pi"], [("cols", 0, 1)])
-    V(1, tc(col(1), P("pg")), ["pg"], [("cols", 1, 2)])
-    V(1, ts(col(2), P("pi"), 1.0, None, A_.is_ge), ["pi"], [("cols", 2, 3)])
-    V(1, ts(col(3), P("pi"), 15.0, None, A_.is_ge), ["pi"], [("cols", 3, 4)])
-    V(1, ts(col(4), col(2), 20.75, -20.0, A_.mult, A_.add), [("cols", 2, 3)], [("cols", 4, 5)])
-    V(1, ts(col(5), P("pi"), 16.0, None, A_.mult), ["pi"], [("cols", 5, 6)])
-    V(1, ts(col(6), P("pg"), 0.0625, None, A_.mult), ["pg"], [("cols", 6, 7)])
-    V(1, tc(col(7), P("wi")), ["wi"], [("cols", 7, 8)])
-    V(1, ts(col(8), P("ki"), 8.0, 2047.5, A_.mult, A_.add), ["ki"], [("cols", 8, 9)])
-    V(1, tc(col(10), P("ki")), ["ki"], [("cols", 10, 11)])
-    V(1, ts(col(9), P("ki"), col(10), -64.0, A_.mult, A_.mult), ["ki", ("cols", 10, 11)], [("cols", 9, 10)])
-    V(1, tc(P("thr", 0, 1), P("li", 0, 1)), ["li"], [("thr", 0, 1)])
-    V(1, ts(P("nth", 0, 1), P("li", 0, 1), -1.0, 0.5, A_.mult, A_.add), ["li"], [("nth", 0, 1)])
-    V(128, ts(P("r15"), P("row"), 15, None, A_.bitwise_and), ["row"], ["r15"])
-    V(128, ts(P("r16"), P("row"), 112, None, A_.bitwise_and), ["row"], ["r16"])
-    c = lambda j: ("cols", j, j + 1)
-    V(128, ts(P("bo"), P("r16"), col(1), None, A_.is_equal), ["r16", c(1)], ["bo"])
-    V(128, ts(P("tq"), P("r15"), 1.0, None, A_.add), ["r15"], ["tq"])
-    V(256, tt(P("qp"), P("tq"), P("bo"), A_.mult), ["tq", "bo"], ["qp"])
-    for i in range(16):
-        V(64, ts(P("ind", 128 * i, 128 * i + 128), P("qp"), float(i + 1), None, A_.is_equal), ["qp"], [("ind", 128 * i, 128 * i + 128)])
-    V(128, ts(P("mk", 0, 128), P("r15"), col(0), None, A_.is_equal), ["r15", c(0)], [("mk", 0, 128)])
-    V(1, lambda e, T: e.memset(T.mk[:, 128:136], 1.0), [], [("mk", 128, 136)])
-    V(128, ts(P("bom", 0, 128), P("bo"), col(2), None, A_.mult), ["bo", c(2)], [("bom", 0, 128)])
-    V(1, tc(P("bom", 128, 129), col(3)), [c(3)], [("bom", 128, 129)])
-    V(64, ts(P("boi"), P("bo"), col(0), None, A_.mult), ["bo", c(0)], ["boi"])
-    V(64, ts(P("wb"), P("bo"), col(7), None, A_.mult), ["bo", c(7)], ["wb"])
-    V(256, tt(P("idb"), P("bo"), P("mk", 0, 128), A_.mult), ["bo", ("mk", 0, 128)], ["idb"])
-    S(128, lambda e, T: e.activation(T.nid[:, :], T.idb[:, :], F_.Copy, scale=-1.0), ["idb"], ["nid"])
-    S(128, lambda e, T: e.activation(T.idf[:, :], T.idb[:, :], F_.Copy), ["idb"], ["idf"])
-    V(128, ts(P("r0f"), P("qp"), 1.0, None, A_.is_equal), ["qp"], ["r0f"])
-    V(128, tc(P("irow"), P("r15")), ["r15"], ["irow"])
-    V(64, ts(P("cs", 0, 8), P("cr", 0, 8), col(6), None, A_.is_equal), ["cr", c(6)], [("cs", 0, 8)])
-    V(64, ts(P("cs", 8, 16), P("cr", 0, 8), col(6), 64.0, A_.is_equal, A_.mult), ["cr", c(6)], [("cs", 8, 16)])
-    V(64, ts(P("g8"), P("cr", 0, 8), col(6), 16.0, A_.is_equal, A_.mult), ["cr", c(6)], ["g8"])
-    V(64, ts(P("cv", 0, 8), P("cr", 0, 8), 256.0, col(5), A_.mult, A_.add), ["cr", c(5)], [("cv", 0, 8)])
-    V(64, ts(P("cv", 8, 16), P("cw", 0, 8), col(0), None, A_.add), ["cw", c(0)], [("cv", 8, 16)])
-    V(64, ts(P("cvs"), P("cr"), 256.0, col(5), A_.mult, A_.add), ["cr", c(5)], ["cvs"])
-    V(64, tc(P("kof"), P("koi")), ["koi"], ["kof"])
-    V(128, ts(P("bm"), P("qp"), 2.0, col(2), A_.is_ge, A_.mult), ["qp", c(2)], ["bm"])
-    for y in range(1, 16):
-        GP(256, lambda e, T, y=y: e.affine_select(T.sh[:, 128 * (y - 1):128 * y], T.bm[:, :], [[-16, 8], [1, 16]], A_.is_equal, 0.0, -(y + 1), 1), ["bm"], [("sh", 128 * (y - 1), 128 * y)])
-    S(2048, lambda e, T: e.activation(T.wr[:, :], T.ind[:, :], F_.Copy, scale=T.cols[:, 7:8]), ["ind", c(7)], ["wr"])
-    V(64, ts(P("csf", 0, 8), P("cr", 0, 8), col(6), None, A_.is_equal), ["cr", c(6)], [("csf", 0, 8)])
-    V(64, ts(P("csf", 8, 16), P("cr", 0, 8), col(6), None, A_.is_equal), ["cr", c(6)], [("csf", 8, 16)])
-    V(64, lambda e, T: e.memset(T.cvf[:, 0:8], -7.5), [], [("cvf", 0, 8)])
-    V(64, ts(P("cvf", 8, 16), P("cr", 0, 8), 256.0, col(5), A_.mult, A_.add), ["cr", c(5)], [("cvf", 8, 16)])
+    def c(j):
+        return ("cols", j, j + 1)
 
-    def mm(e, out, l, r, st, sp):
-        return e.matmul(out, l, r, st, sp)
+    def mms(items, first=True, last=True):
+        return lambda e, T: [e.matmul(o(T), l(T), r(T), first and k == 0, last and k == len(items) - 1) for k, (o, l, r) in enumerate(items)]
+
+    def row(name, k, a, b):
+        return lambda T: T[name][0:k, a:b]
+
+    def blk(name, i):
+        return P(name, 128 * i, 128 * i + 128)
+
+    XS = ("xs", 0, 4096)
+    ev("dx", 16, "xs", "load"); ev("dt", 16, "l0", 3.0); ev("dw", 16, "wi", 2.5); ev("dk", 16, "ki", 2.5); ev("dl", 16, "li", 2.5)
+    GP(2, lambda e, T: e.iota(T.pc[:, :], [[0, 1]], 0, 1), [], ["pc"])
+    def select(out, src, pattern, op, base, mul, n=128):
+        GP(2 * n, lambda e, T: e.affine_select(P(*out)(T), P(*src)(T), pattern, op, 0.0, base, mul), [src], [out])
+
+    def fillc(name, cyc, v, step=None):
+        C(cyc, lambda e, T: e.memset(T[name][:, 0::step] if step else T[name][:, :], v), [], [name])
+
+    def spots(name, k):
+        add("c", "S", {"S": ("s", 700)}, lambda e, T: [e.activation(T[name][:, 16 * j:min(16 * j + 129 * 16, 2048):129], T.ones[:, 0:16], F_.Copy, scale=T[k][:, j:j + 1]) for j in range(8)], ["ones", k], [name])
+
+    GP(32, lambda e, T: e.iota(T.cr[:, :], [[1, 16]], 0, 0, allow_small_or_imprecise_dtypes=True), [], ["cr"])
+    GP(256, lambda e, T: e.iota(T.krow[:, :], [[0, 8], [128, 16]], 0, 0, allow_small_or_imprecise_dtypes=True), [], ["krow"])
+    GP(256, lambda e, T: e.iota(T.krow[0:1, :], [[16, 8], [0, 16]], 0, 0, allow_small_or_imprecise_dtypes=True), [], ["krow"])
+    fillc("ones", 1024, 1.0)
+    fillc("ind", 1024, 0.0)
+    O, G16 = ("ones", 0, 128), [[-16, 8], [0, 16]]
+    select(("up", 0, 128), O, G16, A_.is_ge, 0, 1)
+    select(("bo", 0, 128), ("up", 0, 128), [[16, 8], [0, 16]], A_.is_ge, 15, -1)
+    select(("idb", 0, 128), O, [[-1, 128]], A_.is_equal, 0, 1)
+    C(1, ts(P("pi"), P("pc"), 15, None, A_.bitwise_and), ["pc"], ["pi"])
+    fillc("wr", 1024, 0.0)
+    C(1, tc(col(0), P("pi")), ["pi"], [c(0)])
+    C(1, ts(col(2), P("pi"), 1.0, None, A_.is_ge), ["pi"], [c(2)])
+    C(1, ts(P("s15"), P("pi"), 15.0, None, A_.is_ge), ["pi"], ["s15"])
+    fillc("rst", 512, 0.0)
+    C(1, tc(col(7), P("wi")), ["wi"], [c(7)])
+    C(1, tc(col(10), P("ki")), ["ki"], [c(10)])
+    C(1, tc(P("thr", 0, 1), P("li", 0, 1)), ["li"], [("thr", 0, 1)])
+    fillc("rst", 64, 1024.0, 16)
+    C(1, ts(col(9), P("ki"), col(10), -64.0, A_.mult, A_.mult), ["ki", c(10)], [c(9)])
+    fillc("rs2", 128, 0.0)
+    S("c", 8, act(P("gs"), P("bo", 0, 128, 16), F_.Copy), ["bo"], ["gs"])
+    S("c", 128, act(P("bm"), P("bo"), F_.Copy, 0.0, 1.0 / 2048), ["bo"], ["bm"])
+    spots("ind", "gs")
+    S("c", 1, act(col(3), col(2), F_.Copy, 0.0, 128.0), [c(2)], [c(3)])
+    S("c", 1, act(col(4), col(2), F_.Identity, -20.0, 20.75), [c(2)], [c(4)])
+    S("c", 1, act(col(5), col(0), F_.Copy, 0.0, 16.0), [c(0)], [c(5)])
+    S("c", 8, act(P("gw"), P("gs"), F_.Copy, 0.0, col(7)), ["gs", c(7)], ["gw"])
+    S("c", 1, act(col(8), col(10), F_.Copy, 0.0, 8.0), [c(10)], [c(8)])
+    S("c", 1, act(P("nth", 0, 1), P("thr", 0, 1), F_.Identity, 0.5, -1.0), [("thr", 0, 1)], [("nth", 0, 1)])
+    spots("wr", "gw")
+    for k in range(4 - RV, 4):
+        select(("sh", 128 * k, 128 * k + 128), ("bm", 0, 128), [[-16, 8], [1, 16]], A_.is_equal, -(13 + k), 1)
+        TE("c", 256, mms([(P("q7", k, k + 1), blk("sh", k), col(9))]), [("sh", 128 * k, 128 * k + 128), c(9)], [("q7", k, k + 1)])
+    select(("up", 0, 128), ("bo", 0, 128), [[-1, 128]], A_.is_equal, -1, 1)
+    S("c", 128, act(P("nid"), P("idb"), F_.Copy, 0.0, -1.0), ["idb"], ["nid"])
+    S("c", 128, act(P("nif"), P("idb"), F_.Copy, 0.0, -1.0), ["idb"], ["nif"])
+    for b in (0, 1):
+        for j, (a0, mul, k) in enumerate(((0, 256.0, 5), (0, 16.0, 0), (8 * b, 256.0, 5))):
+            w = ("cv", 24 * b + 8 * j, 24 * b + 8 * j + 8)
+            S("c", 8, act(P(*w), P("cr", a0, a0 + 8), F_.Identity, col(k), mul), ["cr", c(k)], [w])
+    for k in range(4 - RV, 4):
+        S("c", 1, act(col(12 + k), P("q7", k, k + 1), F_.Copy, 0.0, -1.0), [("q7", k, k + 1)], [c(12 + k)])
+    fillc("rs2", 64, 16777216.0, 16)
+    C(256, tt(P("dm"), P("idb"), P("up"), A_.subtract), ["idb", "up"], ["dm"])
+    for b in (1 - TAIL, TAIL):
+        GP(4096, lambda e, T, b=b: e.iota(T["cw%d" % b][:, :], [[0, 2048]], 0, 0), [], ["cw%d" % b])
+        if b != TAIL:
+            select(("ex", 0, 2048), ("ones", 0, 2048), [[-1, 128], [0, 16]], A_.is_equal, 0, 1, 2048)
 
     for t in range(RO):
-        first = len(ops)
+        last = t == RO - 1
         for b in (1 - TAIL, TAIL):
-            tag(ops, first, 1 - b)
-            first = len(ops)
+            now["t"], now["b"] = t, "AB"[b == TAIL]
             sb = str(b)
-            QA, QB, QC, QD = "q%d" % (2 * b), "q%d" % (2 * b + 1), "q%d" % (4 + 2 * b), "q%d" % (5 + 2 * b)
+            QA, QB = "q%d" % (2 * b), "q%d" % (2 * b + 1)
             o = 2048 * b
+            B = lambda n, *a, sb=sb: P(n + sb, *a)
             if t == 0:
-                off = lambda v0, v1, b=b: P("lo0", 128 * b + v0, 128 * b + v1)
-                V(128, tc(P("lo0", 128 * b, 128 * b + 128), P("l0", 128 * b, 128 * b + 128)), [("l0", 128 * b, 128 * b + 128)], [("lo0", 128 * b, 128 * b + 128)])
                 ob = ("lo0", 128 * b, 128 * b + 128)
-                V(128, tc(P("lf" + sb), P("l0", 128 * b, 128 * b + 128)), [("l0", 128 * b, 128 * b + 128)], ["lf" + sb])
+                src = ("l0", 128 * b, 128 * b + 128)
+                V("lo", 128, tc(P(*ob), P(*src)), [src], [ob])
+                S("zs", 1920, lambda e, T, sb=sb: e.activation(T["sk" + sb][96:128, 0:1920], T.ones[96:128, 0:1920], F_.Copy), ["ones"], [("sk" + sb, 0, 1920)])
             else:
                 ln = "land%d%d" % (t, b)
-                ops.append(dict(q="E", c=0.0, fn=("a%d%d" % (t, b), NE), rd=[], wr=R([ln]), n=0, late=4.5 if b else 2.8, after=(t - 1, b)))
-                off = lambda v0, v1, ln=ln: P(ln, v0, v1)
-                ob = at(ln)
-                V(128, tc(P("lf" + sb), P(ln)), [ln], ["lf" + sb])
-
+                ev("a%d%d" % (t, b), 8, ln, "far" if b else "near", (t - 1, b))
+                src = ob = at(ln)
+            V("lq", 128, ts(B("lq"), P(*src), 16.0, col(9), A_.mult, A_.add), [src, c(9)], ["lq" + sb])
+            for k in range(4 - RV, 4):
+                TE("rev%d" % k, 512, mms([(blk(QB, k), blk("sh", k), B("lq"))]), [("sh", 128 * k, 128 * k + 128), "lq" + sb], [(QB, 128 * k, 128 * k + 128)])
+            for k in range(4 - RV, 4):
+                S("rcp%d" % k, 128, act(blk("sk" + sb, 12 + k), blk(QB, k), F_.Identity, col(12 + k)), [(QB, 128 * k, 128 * k + 128), c(12 + k)], [("sk" + sb, 128 * (12 + k), 128 * (13 + k))])
+            for lv, (w, y0) in enumerate(((1, 15), (4, 12))):
+                if w >= RV:
+                    add("sh%d" % lv, "Y", {"Y": ("y", 3)},
+                        lambda e, T, w=w, y0=y0, sb=sb: [e.dma_start(T["sk" + sb][0:128 - s, 128 * (y0 - s):128 * (y0 - s + w)], T["sk" + sb][s:128, 128 * y0:128 * (y0 + w)]) for s in (w, 2 * w, 3 * w)],
+                        [("sk" + sb, 128 * y0, 128 * (y0 + w))], [("sk" + sb, 128 * (y0 - 3 * w), 128 * y0)], late="dma", sem="r%d%d" % (lv, b))
+            CH = OPT["C1"][b == TAIL]
             for v0 in range(0, 128, CH):
                 c0, c1 = o + 16 * v0, o + 16 * (v0 + CH)
-                gat(add, "gg", c0, c1, off(v0, v0 + CH), ob)
-                V((c1 - c0) // 2, lambda e, T, c0=c0, c1=c1: e.tensor_tensor_scan(T.mm[:, c0:c1], T.rst[:, 0:c1 - c0], T.gg[:, c0:c1], 0.0, A_.add, A_.min),
-                  ["rst", ("gg", c0, c1)], [("mm", c0, c1)])
-                held(add, c0, c1, t)
-                TE(16 * 64, lambda e, T, v0=v0, c0=c0, c1=c1, QA=QA, CH=CH: [e.matmul(T[QA][:, v0:v0 + CH], T.ind[:, 128 * i:128 * i + 128], T.hb[:, c0 + i:c1:16], i == 0, i == 15) for i in range(16)],
-                   ["ind", ("hb", c0, c1)], [(QA, v0, v0 + CH)], 16)
-            S(128, lambda e, T, sb=sb: e.activation(T["lq" + sb][:, :], T["lf" + sb][:, :], F_.Identity, bias=T.cols[:, 9:10], scale=16.0), ["lf" + sb, c(9)], ["lq" + sb])
-            S(64, lambda e, T, sb=sb, QD=QD: e.activation(T[QD][:, 0:64], T["lf" + sb][:, 0:64], F_.Copy, scale=4096.0), ["lf" + sb], [(QD, 0, 64)])
-            V(64, tt(P("lp" + sb), P("lf" + sb, 64, 128), P(QD, 0, 64), A_.add), ["lf" + sb, (QD, 0, 64)], ["lp" + sb])
-            for Q, y0, y1 in ((QC, 1, 8), (QD, 8, 16)):
-                n = y1 - y0
-                TE(n * 256, lambda e, T, Q=Q, y0=y0, y1=y1, sb=sb: [e.matmul(T[Q][:, 64 * (y - y0):64 * (y - y0) + 64], T.sh[:, 128 * (y - 1):128 * y], T["lp" + sb][:, :], True, True) for y in range(y0, y1)],
-                   ["sh", "lp" + sb], [(Q, 0, 64 * n)], n)
-                S(64 * n, lambda e, T, Q=Q, n=n, y0=y0, sb=sb: e.activation(T["sk" + sb][:, 64 * y0:64 * y0 + 64 * n], T[Q][:, 0:64 * n], F_.Copy), [(Q, 0, 64 * n)], [("sk" + sb, 64 * y0, 64 * y0 + 64 * n)])
-            V(128, ts(P("ok" + sb), P(QA, 0, 128), col(4), None, A_.is_ge), [(QA, 0, 128), c(4)], ["ok" + sb])
-            TE(129, lambda e, T, sb=sb, QA=QA: [e.matmul(T[QA][:, 128:257], T["ok" + sb][:, :], T.bom[:, 0:129], True, True)], ["ok" + sb, ("bom", 0, 129)], [(QA, 128, 257)])
-            V(129, tt(P("ms" + sb, 0, 129), P("mk", 0, 129), P(QA, 128, 257), A_.mult), ["mk", (QA, 128, 257)], [("ms" + sb, 0, 129)])
-            TE(128, lambda e, T, sb=sb, QA=QA: [e.matmul(T[QA][:, 264:280], T["ms" + sb][:, 0:128], T.cs[:, :], True, False), e.matmul(T[QA][:, 264:280], T.idb[:, :], T.cv[:, :], False, True)],
-               [("ms" + sb, 0, 129), "cs", "idb", "cv"], [(QA, 264, 280)], 2)
-            V(64, tc(P("ofm" + sb), P(QA, 264, 280)), [(QA, 264, 280)], ["ofm" + sb])
-            gat(add, "xl", 128 * b, 128 * b + 128, P("ofm" + sb, 0, 8), ("ofm" + sb, 0, 16), ("gg", o, o + 2048))
-            gat(add, "zz", 128 * b, 128 * b + 128, P("ofm" + sb, 0, 8), ("ofm" + sb, 0, 16), ("mm", o, o + 2048))
-            TE(192, lambda e, T, b=b, QB=QB: [e.matmul(T[QB][:, 0:128], T.wb[:, :], T.xl[:, 128 * b:128 * b + 128], True, False), e.matmul(T[QB][:, 0:128], T.kc[0:2, :], T.ones[0:2, 0:128], False, True)],
-               ["wb", ("xl", 128 * b, 128 * b + 128), "kc", "ones"], [(QB, 0, 128)], 2)
-            V(128, ts(P("rr" + sb), P(QB, 0, 128), BIG, BIG, A_.add, A_.subtract), [(QB, 0, 128)], ["rr" + sb])
-            V(128, tt(P("ww" + sb), P(QB, 0, 128), P("rr" + sb), A_.subtract), [(QB, 0, 128), "rr" + sb], ["ww" + sb])
-            S(128, lambda e, T, sb=sb, QB=QB: e.activation(T[QB][:, 128:256], T["ww" + sb][:, :], F_.Square, bias=T.cols[:, 8:9]), ["ww" + sb, c(8)], [(QB, 128, 256)])
-            V(128, tt(P("ci" + sb), P("lq" + sb), P(QB, 128, 256), A_.add), ["lq" + sb, (QB, 128, 256)], ["ci" + sb])
-            V(128, ts(P("cc" + sb), P("ci" + sb), 4, 4095, A_.arith_shift_right, A_.bitwise_and), ["ci" + sb], ["cc" + sb])
-            V(128, tc(P("ofc" + sb), P("cc" + sb)), ["cc" + sb], ["ofc" + sb])
-            TE(128, lambda e, T, b=b, QD=QD: [e.matmul(T[QD][:, 0:128], T.zz[:, 128 * b:128 * b + 128], T.nid[:, :], True, True)], [("zz", 128 * b, 128 * b + 128), "nid"], [(QD, 0, 128)])
-            S(128, lambda e, T, sb=sb, QD=QD: e.activation(T["zt" + sb][:, :], T[QD][:, 0:128], F_.Copy), [(QD, 0, 128)], ["zt" + sb])
+                k = str(v0 // CH)
+                gat("g1" + k, ("gg", c0, c1), XS, (ob[0], ob[1] + v0, ob[1] + v0 + CH))
+                V("sc" + k, 8 * CH, scan(P("mm", c0, c1), P("rst", 0, c1 - c0), P("gg", c0, c1)), ["rst", ("gg", c0, c1)], [("mm", c0, c1)])
+                VS("hb" + k, 8 * CH, 16 * CH, ts(P("hb", c0, c1), P("mm", c0, c1), P("thr", t, t + 1), 0.5, A_.is_ge, A_.subtract),
+                   act(P("hb", c0, c1), P("mm", c0, c1), F_.Sign, P("nth", t, t + 1)), [("mm", c0, c1), ("thr", t, t + 1), ("nth", t, t + 1)], [("hb", c0, c1)])
+            for h in (0, 1):
+                c0, c1 = o + 1024 * h, o + 1024 * h + 1024
+                TE("su%d" % h, 1024, mms([(P(QB, 64 * h, 64 * h + 64), blk("wr", i), P("gg", c0 + i, c1, 16)) for i in range(16)]), ["wr", ("gg", c0, c1)], [(QB, 64 * h, 64 * h + 64)])
+                TE("cnt%d" % h, 1024, mms([(P(QA, 64 * h, 64 * h + 64), blk("ind", i), P("hb", c0 + i, c1, 16)) for i in range(16)]), ["ind", ("hb", c0, c1)], [(QA, 64 * h, 64 * h + 64)])
+            V("si", 128, tc(B("si"), P(QB, 0, 128)), [(QB, 0, 128)], ["si" + sb])
+            V("ul", 128, ts(B("uu", 0, 128), B("si"), 15, None, A_.bitwise_and), ["si" + sb], [("uu" + sb, 0, 128)])
+            V("uh", 128, ts(B("uu", 128, 256), B("si"), 4080, None, A_.bitwise_and), ["si" + sb], [("uu" + sb, 128, 256)])
+            ok, okm, pl = (("ok" + sb, 128 * j, 128 * j + 128) for j in range(3))
+            V("ok", 128, ts(P(*ok), P(QA, 0, 128), col(4), None, A_.is_ge), [(QA, 0, 128), c(4)], [ok])
+            TE("last", 256, lambda e, T, QA=QA, ok=ok: [e.matmul(T[QA][:, a:a + 128], T.dm[:, :], P(*ok)(T), True, True) for a in (128, 256)], ["dm", ok], [(QA, 128, 384)])
+            V("pu", 256, tt(B("ok", 256, 512), B("uu"), P(QA, 128, 384), A_.mult), ["uu" + sb, (QA, 128, 384)], [("ok" + sb, 256, 512)])
+            TE("u", 256, mms([(P(QB, 128, 256), P("bo"), B("ok", a, a + 128)) for a in (256, 384)]), ["bo", ("ok" + sb, 256, 512)], [(QB, 128, 256)])
+            VS("okm", 64, 128, ts(P(*okm), P(*ok), col(3), None, A_.mult), act(P(*okm), P(*ok), F_.Copy, 0.0, col(3)), [ok, c(3)], [okm])
+            nw = 16 if last else 24
+            W = P(QA, 384, 384 + nw)
+            TE("wm", 18 * 64, mms([(W, P("idb"), P("cv", 24 * b, 24 * b + nw)), (P(QA, 384, 392), P("nid"), P("ones", 0, 8))] +
+                                  [(W, blk("ind", r), B("ok", r, 16 * nw, 16)) for r in range(16)]),
+               ["idb", "cv", "ones", "nid", "ind", ("ok" + sb, 0, 16 * nw)], [(QA, 384, 384 + nw)])
+            V("ofm", 24, tc(B("ofm", 0, nw), W), [(QA, 384, 384 + nw)], ["ofm" + sb])
+            S("sq", 128, act(P(QB, 256, 384), P(QB, 128, 256), F_.Square, col(8)), [(QB, 128, 256), c(8)], [(QB, 256, 384)])
+            V("ci", 128, tt(B("ci"), B("lq"), P(QB, 256, 384), A_.add), ["lq" + sb, (QB, 256, 384)], ["ci" + sb])
+            V("cc", 128, ts(B("cc"), B("ci"), 4, 4095, A_.arith_shift_right, A_.bitwise_and), ["ci" + sb], ["cc" + sb])
+            V("ofc", 128, tc(B("ofc"), B("cc")), ["cc" + sb], ["ofc" + sb])
+            add("cw", "Y", {"Y": ("y", 1)}, lambda e, T, sb=sb: [e.dma_start(T["cw" + sb][0:128:16, :], T["cc" + sb][:, :])], ["cc" + sb], ["cw" + sb], late="dma", sem="w" + sb)
+            gat("gz", ("zz" + sb, 0, 128), ("mm", o, o + 2048), ("ofm" + sb, 0, 8), 0.5, -0.25)
+            TE("zt", 512, mms([(P(QA, 0, 128), B("zz"), P("nif"))]), ["zz" + sb, "nif"], [(QA, 0, 128)])
+            S("zc", 128, act(B("zt"), P(QA, 0, 128), F_.Identity, -0.25), [(QA, 0, 128)], ["zt" + sb])
+            TE("nok", 256, mms([(P(QA, 128, 256), P("nid"), P(*ok)), (P(QA, 128, 256), row("ones", 1, 0, 128), row("ones", 1, 0, 128))]), ["nid", ok, "ones"], [(QA, 128, 256)])
+            VG("rv", 128, tt(B("rv"), by(("sk" + sb,), ("ofm" + sb, 8, 16)), P(*okm), A_.mult), ["sk" + sb, ("ofm" + sb, 8, 16), okm], ["rv" + sb])
+            V("cm", 128, tt(P(QA, 256, 384), B("cc"), P(QA, 128, 256), A_.mult), ["cc" + sb, (QA, 128, 256)], [(QA, 256, 384)])
+            V("rest", 128, tt(B("cm"), B("rv"), P(QA, 256, 384), A_.add), ["rv" + sb, (QA, 256, 384)], ["cm" + sb])
+            if b == TAIL and not last:
+                TE("cut", 128, mms([(P(QA, 408, 409), P("ok%d" % j, 0, 128), P("s15")) for j in (0, 1)]), [("ok0", 0, 128), ("ok1", 0, 128), "s15"], [(QA, 408, 409)])
+                S("cn", 1, act(P("cn"), P(QA, 408, 409), F_.Copy), [(QA, 408, 409)], ["cn"])
+                TE("cut2", 64, mms([(P(QA, 409, 410), P("ones", 0, 128), P("cn"))]), ["ones", "cn"], [(QA, 409, 410)])
+                V("ei", 1, ts(P("ei"), P(QA, 409, 410), -1.0, 2048.0, A_.mult, A_.add), [(QA, 409, 410)], ["ei"])
+                V("ea", 1, ts(P("ea"), P("ei"), 7, None, A_.bitwise_and), ["ei"], ["ea"])
+                V("thr", 1, tt(P("thr", t + 1, t + 2), P("li", t + 1, t + 2), P("ea"), A_.add), ["li", "ea"], [("thr", t + 1, t + 2)])
+                S("nth", 1, act(P("nth", t + 1, t + 2), P("thr", t + 1, t + 2), F_.Identity, 0.5, -1.0), [("thr", t + 1, t + 2)], [("nth", t + 1, t + 2)])
             for k in range(4):
-                Q = (QC, QD)[k % 2]
+                Q = "q%d" % (4 + k)
                 c0, c1 = o + 512 * k, o + 512 * k + 512
-                gat(add, "hh", c0, c1, P("ofc" + sb, 32 * k, 32 * k + 32), ("ofc" + sb, 0, 128))
-                TE(1024, lambda e, T, Q=Q, c0=c0, c1=c1, k=k, sb=sb: [e.matmul(T[Q][:, :], T["zt" + sb][:, :], T.ex[:, 512 * k:512 * k + 512], True, False), e.matmul(T[Q][:, :], T.idb[:, :], T.hh[:, c0:c1], False, True)],
-                   ["zt" + sb, "ex", "idb", ("hh", c0, c1)], [Q], 2)
-                S(512, lambda e, T, Q=Q, c0=c0, c1=c1: e.activation(T.aa[:, c0:c1], T[Q][:, :], F_.Abs), [Q], [("aa", c0, c1)])
-            V(270, lambda e, T, sb=sb: e.tensor_copy(T["rp" + sb][:, :], T["sk" + sb][:, :].indirect(T["ofm" + sb][:, 8:16])), ["sk" + sb, ("ofm" + sb, 0, 16)], ["rp" + sb])
-            V(64, ts(P("rv" + sb, 0, 64), P("rp" + sb, 0, 64), 12, None, A_.arith_shift_right), ["rp" + sb], [("rv" + sb, 0, 64)])
-            V(64, ts(P("rv" + sb, 64, 128), P("rp" + sb, 64, 128), 4095, None, A_.bitwise_and), ["rp" + sb], [("rv" + sb, 64, 128)])
-            TE(256, lambda e, T, sb=sb, QA=QA: [e.matmul(T[QA][:, 280:408], T.nid[:, :], T["ok" + sb][:, :], True, False), e.matmul(T[QA][:, 280:408], T.ones[0:1, 0:128], T.ones[0:1, 0:128], False, True)],
-               ["nid", "ok" + sb, "ones"], [(QA, 280, 408)], 2)
-            V(128, tt(P(QA, 0, 128), P("cc" + sb), P(QA, 280, 408), A_.mult), ["cc" + sb, (QA, 280, 408)], [(QA, 0, 128)])
-            V(128, tt(P("rest" + sb), P("rv" + sb), P(QA, 0, 128), A_.add), ["rv" + sb, (QA, 0, 128)], ["rest" + sb])
-            TE(16 * 64 + 128, lambda e, T, o=o, QB=QB: [e.matmul(T[QB][:, 384:512], T.ones[0:1, 0:128], T.irow[0:1, :], True, False)] +
-               [e.matmul(T[QB][:, 384 + i:512:16], T.aa[:, o + i:o + 2048:16], T.g8[:, :], False, i == 15) for i in range(16)],
-               ["ones", "irow", ("aa", o, o + 2048), "g8"], [(QB, 384, 512)], 17)
-            V(128, lambda e, T, sb=sb, QB=QB: e.tensor_tensor_scan(T["ks" + sb][:, :], T.rs2[:, :], T[QB][:, 384:512], 0.0, A_.add, A_.min), ["rs2", (QB, 384, 512)], ["ks" + sb])
-            V(270, lambda e, T, sb=sb: e.tensor_copy(T["kr" + sb][:, :], T["ks" + sb][:, :].indirect(T.kof[:, :])), ["ks" + sb, "kof"], ["kr" + sb])
-            V(128, tt(P("oh" + sb), P("kr" + sb), P(QB, 384, 512), A_.is_equal), ["kr" + sb, (QB, 384, 512)], ["oh" + sb])
-            TE(128, lambda e, T, sb=sb, QA=QA: [e.matmul(T[QA][:, 0:128], T["oh" + sb][:, :], T.idb[:, :], True, True)], ["oh" + sb, "idb"], [(QA, 0, 128)])
-            V(128, tt(P("pb" + sb), P("cc" + sb), P(QA, 0, 128), A_.mult), ["cc" + sb, (QA, 0, 128)], ["pb" + sb])
-            TE(512, lambda e, T, sb=sb, QD=QD: [e.matmul(T[QD][:, 0:128], T.idf[:, :], T["rest" + sb][:, :], True, False)], ["idf", "rest" + sb], [(QD, 0, 128)])
-            TE(512, lambda e, T, sb=sb, QD=QD: [e.matmul(T[QD][:, 0:128], T.r0f[:, :], T["pb" + sb][:, :], False, True)], ["r0f", "pb" + sb], [(QD, 0, 128)])
-            if t < RO - 1:
+                gat("g2%d" % k, ("hh", c0, c1), XS, ("ofc" + sb, 32 * k, 32 * k + 32), 0.5)
+                TE("sub%d" % k, 1024, mms([(P(Q), B("zt"), P("ex", 512 * k, 512 * k + 512)), (P(Q), P("idb"), P("hh", c0, c1))]), ["zt" + sb, "ex", "idb", ("hh", c0, c1)], [Q])
+                S("ab%d" % k, 512, act(lambda T, c0=c0, c1=c1: T.aa[:, c0 // 256:c1 // 256, :, :], P(Q), F_.Abs, 0.0, 4096.0), [Q], [("aa", c0, c1)])
+                if k % 2:
+                    h = k // 2
+                    items = [(P(QB, 64 * h, 64 * h + 64), blk("ind", r), lambda T, r=r, a=8 * b + 4 * h: T.aa[:, a:a + 4, r, :]) for r in range(16)]
+                    if h == 0:
+                        items = [(P(QB, 0, 128), row("ones", 2, 0, 128), row("krow", 2, 0, 128))] + items
+                    TE("kp%d" % h, 1024 + 128 * (h == 0), mms(items, h == 0, h == 1), ["ones", "krow", "ind", ("aa", c1 - 1024, c1)], [(QB, 0, 128)])
+            V("kw", 128, scan(B("kw"), P("rs2"), P(QB, 0, 128)), ["rs2", (QB, 0, 128)], ["kw" + sb])
+            V("ka", 8, tc(B("ka"), B("kw", 15, 128, 16)), ["kw" + sb], ["ka" + sb])
+            V("kb", 8, ts(B("kb"), B("ka"), 2047, None, A_.bitwise_and), ["ka" + sb], ["kb" + sb])
+            V("ofl", 8, ts(B("ofl"), B("kb"), col(0), None, A_.add), ["kb" + sb, c(0)], ["ofl" + sb])
+            VG("new", 128, tt(B("out"), by(("cw" + sb,), ("ofl" + sb,)), B("cm"), A_.add), ["cw" + sb, "ofl" + sb, "cm" + sb], ["out" + sb])
+            if not last:
                 nb = "nb%d%d" % (t + 1, b)
-                V(128, tc(P(nb), P(QD, 0, 128)), [(QD, 0, 128)], [nb])
-                ops.append(dict(q="G", c=1.0, fn=None, rd=R([nb]), wr=[], n=0, late=0.0, send=(t, b, nb)))
-                if b == TAIL:
-                    V(256, tt(P("km"), P("kr" + sb), P("mk", 0, 128), A_.mult), ["kr" + sb, ("mk", 0, 128)], ["km"])
-                    TE(512, lambda e, T, QA=QA: [e.matmul(T[QA][:, 264:280], T.idf[:, :], T.cvf[:, :], True, False), e.matmul(T[QA][:, 264:280], T.km[:, :], T.csf[:, :], False, True)],
-                       ["km", "csf", "idf", "cvf"], [(QA, 264, 280)], 2)
-                    V(8, ts(P("kq"), P(QA, 264, 272), BIG16, BIG16, A_.add, A_.subtract), [(QA, 264, 280)], ["kq"])
-                    V(8, tt(P("kd"), P(QA, 272, 280), P("kq"), A_.subtract), [(QA, 264, 280), "kq"], ["kd"])
-                    V(8, tc(P("ofi" + sb), P("kd")), ["kd"], ["ofi" + sb])
-                else:
-                  S(128, lambda e, T, sb=sb, QA=QA: e.activation(T["ot" + sb][:, :], T[QA][:, 0:128], F_.Copy), [(QA, 0, 128)], ["ot" + sb])
-                  TE(128, lambda e, T, sb=sb, QA=QA: [e.matmul(T[QA][:, 128:256], T["ot" + sb][:, :], T.boi[:, :], True, True)], ["ot" + sb, "boi"], [(QA, 128, 256)])
-                  V(128, tt(P("mt" + sb), P("mk", 0, 128), P(QA, 128, 256), A_.mult), ["mk", (QA, 128, 256)], ["mt" + sb])
-                  TE(128, lambda e, T, sb=sb, QA=QA: [e.matmul(T[QA][:, 264:272], T["mt" + sb][:, :], T.cs[:, 0:8], True, False), e.matmul(T[QA][:, 264:272], T.idb[:, :], T.cv[:, 0:8], False, True)],
-                   ["mt" + sb, "cs", "idb", "cv"], [(QA, 264, 272)], 2)
-                  V(64, tc(P("ofi" + sb), P(QA, 264, 272)), [(QA, 264, 272)], ["ofi" + sb])
-                h0, h1 = 128 * b, 128 * b + 128
-                V(270, lambda e, T, sb=sb, o=o, h0=h0, h1=h1: e.tensor_tensor(T.yi[:, h0:h1], T.hh[:, o:o + 2048].indirect(T["ofi" + sb][:, :]), T.zz[:, h0:h1], A_.add),
-                  [("hh", o, o + 2048), "ofi" + sb, ("zz", h0, h1)], [("yi", h0, h1)])
-                V(128, ts(P("y2", h0, h1), P("yi", h0, h1), 1, None, A_.arith_shift_right), [("yi", h0, h1)], [("y2", h0, h1)])
+                V("nb", 128, tc(P(nb), B("out")), ["out" + sb], [nb])
+                add("send", "G", {"G": ("i", 0)}, None, [nb], [], send=(t, b, nb))
+                V("ki", 8, ts(B("kc"), B("ka"), 7, 15, A_.arith_shift_right, A_.bitwise_and), ["ka" + sb], ["kc" + sb])
+                V("kj", 8, tt(B("kd"), B("kc"), P("cv", 0, 8), A_.add), ["kc" + sb, ("cv", 0, 8)], ["kd" + sb])
+                V("ofi", 8, tc(B("ofi"), B("kd")), ["kd" + sb], ["ofi" + sb])
+                VG("yi", 128, tt(B("yi"), by(("hh", o, o + 2048), ("ofi" + sb,)), B("zz"), A_.add), [("hh", o, o + 2048), "ofi" + sb, "zz" + sb], ["yi" + sb])
             else:
-                h0, h1 = 128 * b, 128 * b + 128
-                V(128, tc(P("out" + sb), P(QD, 0, 128)), [(QD, 0, 128)], ["out" + sb])
-                S(128, lambda e, T, sb=sb, h0=h0, h1=h1: e.activation(T["zo" + sb][:, :], T.zz[:, h0:h1], F_.Copy), [("zz", h0, h1)], ["zo" + sb])
-                ops.append(dict(q="Y", c=0.1, fn=("yz", h0, h1, "zo" + sb, "o0" + sb), rd=R(["zo" + sb]), wr=[], n=0, late=2.0))
-                ops.append(dict(q="Y", c=0.1, fn=("yl", h0, h1, "out" + sb, "o1" + sb), rd=R(["out" + sb]), wr=[], n=0, late=2.0))
-        tag(ops, first, TAIL)
-        if t < RO - 1:
-            TE(128, lambda e, T: [e.matmul(T.q0[:, 408:409], T.ones[:, 0:128], T.ms1[:, 128:129], True, False), e.matmul(T.q0[:, 408:409], T.ones[:, 0:128], T.ms0[:, 128:129], False, True)],
-               ["ones", ("ms0", 128, 129), ("ms1", 128, 129)], [("q0", 408, 409)], 2)
-            V(1, ts(P("ei"), P("q0", 408, 409), -1.0, 2048.0, A_.mult, A_.add), [("q0", 408, 409)], ["ei"])
-            V(1, ts(P("ea"), P("ei"), 7, None, A_.bitwise_and), ["ei"], ["ea"])
-            V(1, tt(P("thr", t + 1, t + 2), P("li", t + 1, t + 2), P("ea"), A_.add), ["li", "ea"], [("thr", t + 1, t + 2)])
-            V(1, ts(P("nth", t + 1, t + 2), P("thr", t + 1, t + 2), -1.0, 0.5, A_.mult, A_.add), [("thr", t + 1, t + 2)], [("nth", t + 1, t + 2)])
-            TE(16 * 64, lambda e, T: [e.matmul(T.q2[:, 416:432], T.wr[:, 128 * r:128 * r + 128], T.xl[:, r::16], r == 0, r == 15) for r in range(16)], ["wr", "xl"], [("q2", 416, 432)], 16)
-            V(64, tc(P("uw"), P("q2", 416, 432)), [("q2", 416, 432)], ["uw"])
-            V(64, ts(P("u15"), P("uw"), 15, None, A_.bitwise_and), ["uw"], ["u15"])
-            V(64, tt(P("uv"), P("u15"), P("cvs"), A_.add), ["u15", "cvs"], ["uv"])
-            V(64, tc(P("ofs"), P("uv")), ["uv"], ["ofs"])
-            for b in (1, 0):
-                V(540, lambda e, T, b=b: e.tensor_copy(T.xs[:, :].indirect(T.ofs[:, 8 * b:8 * b + 8]), T.y2[:, 128 * b:128 * b + 128]),
-                  [("y2", 128 * b, 128 * b + 128), "ofs"], ["xs"])
+                S("zo", 128, act(B("zo"), B("zz"), F_.Identity, 0.5, 2.0), ["zz" + sb], ["zo" + sb])
+                for k, (dst, src) in enumerate((("yz", "zo"), ("yl", "out"))):
+                    add(dst, "Y", {"Y": ("y", 1)}, lambda e, T, dst=dst, src=src + sb, b=b: [e.dma_start(T[dst][:, 128 * b:128 * b + 128], T[src][:, :])],
+                        [src + sb], [], late=2.0, sem="o%d%d" % (k, b))
+        if not last:
+            for b in (1 - TAIL, TAIL):
+                now["b"] = "AB"[b == TAIL]
+                of = ("ofm%d" % b, 16, 24)
+                VG("put", 128, tc(by(XS, of), P("yi%d" % b)), ["yi%d" % b, of], ["xs"], "sv")
     return ops
 
 
-def tag(ops, first, b):
-    for op in ops[first:]:
-        op["b"] = b
-
-
-def gat(add, dst, c0, c1, off, ob, win=("xs", 0, 4096), q="VS"):
-    def fn(e, T, scalar):
-        src = T[win[0]][:, win[1]:win[2]].indirect(off(T))
-        return [e.activation(T[dst][:, c0:c1], src, F_.Copy) if scalar else e.tensor_copy(T[dst][:, c0:c1], src)]
-    n = c1 - c0
-    add(q, {"V": 0.06 + n * 1.56 * CYC, "S": 0.075 + n * 1.56 * CYC}, fn, [win, ob], [(dst, c0, c1)], 1, 0.0, True)
-
-
-def held(add, c0, c1, t):
-    def fn(e, T, scalar):
-        if scalar:
-            return [e.activation(T.hb[:, c0:c1], T.mm[:, c0:c1], F_.Sign, bias=T.nth[:, t:t + 1])]
-        return [e.tensor_scalar(T.hb[:, c0:c1], T.mm[:, c0:c1], T.thr[:, t:t + 1], 0.5, A_.is_ge, A_.subtract)]
-    n = c1 - c0
-    add("VS", {"V": 0.02 + n * 0.5 * CYC, "S": 0.065 + n * CYC}, fn, [("mm", c0, c1), ("thr", t, t + 1), ("nth", t, t + 1)], [("hb", c0, c1)], 1, 0.0, True)
+def price(kind, n, K):
+    cyc = 0.00083 * K["f"]
+    return {"v": max(64, n) * cyc + K["vfix"], "s": n * cyc + 0.065, "gv": 0.05 + n * K["gat"] * cyc, "gs": 0.065 + n * K["gat"] * cyc,
+            "sv": 0.05 + n * K["sca"] * cyc, "t": n * K["pe"] * K["f"] + 0.03, "g": 0.17 + n * cyc, "y": 0.1 * n, "i": K["issue"], "0": 0.0}[kind]
 
 
 def link(ops):
@@ -343,8 +339,8 @@ def link(ops):
                 if k2 == k:
                     continue
                 over = a < z2 and a2 < z
+                same = op["q"] == ops[k2]["q"] and len(op["q"]) == 1 and op["q"] != "Y"
                 if ps:
-                    same = op["q"] == ops[k2]["q"]
                     if not same:
                         deps.add(k2)
                     elif over and w2 and op["q"] != "T":
@@ -352,12 +348,10 @@ def link(ops):
                     else:
                         order.add(k2)
                 elif over and (wr or w2):
-                    if w2:
+                    if w2 or not same:
                         deps.add(k2)
-                    elif op["q"] == ops[k2]["q"] and len(op["q"]) == 1:
-                        order.add(k2)
                     else:
-                        deps.add(k2)
+                        order.add(k2)
         for (bn, a, z), wr in acc:
             h = hist.setdefault(bn, [])
             if wr and SCRATCH[bn][0] != "psum":
@@ -372,73 +366,104 @@ def link(ops):
         op["deps"], op["order"] = deps, order - deps
 
 
-LAT = 0.17
+def ranks(ops, succ, pos, span):
+    rank = [op["t"] * span + pos.get(op["name"], 0.0) + k * 1e-6 for k, op in enumerate(ops)]
+    for k in range(len(ops) - 1, -1, -1):
+        if ops[k]["t"] < 0:
+            rank[k] = min(rank[x] for x in succ[k]) - 1e-3
+    return rank
 
 
-def schedule(ops, bias=0.0, jit=None):
+def fill(ops, K, pos, span):
     n = len(ops)
     succ = [[] for _ in range(n)]
     left = [0] * n
-    cost = [op["c"] if isinstance(op["c"], dict) else {q: op["c"] for q in op["q"]} for op in ops]
     for k, op in enumerate(ops):
         for d in op["deps"] | op["order"]:
             succ[d].append(k)
             left[k] += 1
-    prio = [0.0] * n
-    for k in range(n - 1, -1, -1):
-        op = ops[k]
-        prio[k] = min(cost[k].values()) + op["late"] + LAT + max([prio[s] for s in succ[k]], default=0.0)
-    prio = [prio[k] + (bias if ops[k].get("b", TAIL) != TAIL else 0.0) + (jit[k] if jit is not None else 0.0) for k in range(n)]
-    free = {"V": 0.0, "S": 0.0, "T": 0.0, "G": 0.0, "Y": 0.0, "E": 0.0}
-    end, est = [None] * n, [0.0] * n
+    rank = ranks(ops, succ, pos, span)
+    busy = {q: [] for q in "VSTGYE"}
+    est, total, lat = [0.0] * n, 0.0, K["lat"]
     ready = [k for k in range(n) if left[k] == 0]
-    seq = []
     while ready:
-        cands = []
-        for k in ready:
-            f, s, q = min((max(est[k], free[q]) + cost[k][q], max(est[k], free[q]), q) for q in ops[k]["q"])
-            cands.append((s, -prio[k], k, q))
-        first = min(cands)[0]
-        s, p, k, q = min((x for x in cands if x[0] <= first + SLACK), key=lambda x: (x[1], x[0], x[3]))
-        op = ops[k]
+        k = min(ready, key=lambda x: rank[x])
         ready.remove(k)
-        op["at"], op["on"], op["cost"] = s, q, cost[k][q]
-        end[k] = s + cost[k][q] + op["late"]
+        op = ops[k]
+        best = None
+        for q in op["q"]:
+            c, s, iv = price(*op["c"][q], K), est[k], busy[q]
+            j = len(iv)
+            while j and iv[j - 1][1] > s:
+                j -= 1
+            while j < len(iv) and iv[j][0] < s + c:
+                s = max(s, iv[j][1])
+                j += 1
+            if best is None or s + c < best[0]:
+                best = (s + c, s, q, j, c)
+        f, s, q, j, c = best
         if q != "E":
-            free[q] = s + cost[k][q]
+            busy[q].insert(j, (s, f))
+        op["at"], op["on"], op["cost"] = s, q, c
+        f += K.get(op.get("late"), op.get("late")) or 0.0
+        total = max(total, f)
+        for x in succ[k]:
+            left[x] -= 1
+            est[x] = max(est[x], f + (lat if k in ops[x]["deps"] else 0.0))
+            if left[x] == 0:
+                ready.append(x)
+    return sorted(range(n), key=lambda k: (ops[k]["at"], k)), total
+
+
+def issue(ops, pos, span):
+    n = len(ops)
+    succ = [[] for _ in range(n)]
+    left = [0] * n
+    for k, op in enumerate(ops):
+        for d in op["deps"] | op["order"]:
+            succ[d].append(k)
+            left[k] += 1
+    rank = [op["t"] * span + pos.get(op["name"], -9 * span) for op in ops]
+    ready, seq = [k for k in range(n) if left[k] == 0], []
+    while ready:
+        k = min(ready, key=lambda x: (rank[x], x))
+        ready.remove(k)
         seq.append(k)
         for x in succ[k]:
             left[x] -= 1
-            est[x] = max(est[x], end[k] + (LAT if k in ops[x]["deps"] else 0.0))
             if left[x] == 0:
                 ready.append(x)
-    return seq, max(end)
+    return seq
 
 
-SLACK = 0.0
 PLAN = {}
-ABC = "0123456789abcdefghijklmnopqrstuvwxyzABCDEFGHIJKLMNOPQRSTUVWXYZ"
-SHIFT = "Hn5HSB0sWoYXui7RA78nABE8EBZzIOZKC14QtTAQZZaTN8ozoDTEzE05yVeOQZTZZTTDOTTMLTTHlTihqMt32TxTFszH3qLsQnMCTxTbAC1AAFnSIh7T43eCeAEDRKyLTxPZVryJAGukDAHffVZZLQcXxUWtpyink8jZVuC9PQZdHZZYodZLCzvutVWZmoQVsHZBZZcsZmjUkRZdUttAmPX5xZAZPi05ZC01Q3YEd19aQtdyB7qdlI8YjKVUUbxYZfYwN3u6TRLDsNYMG4uZV0fVVM0xg0vEdcJeubm2Goyb0M3bst0DjWRnRMOCj0KnfOqXV10gdDjq0yiulFSPO2SQKX5ZOZnOPQCbXOlanw5o5fpv580Sa5u5g7f1v0yRKScQDoQFtpIZJrxANUysEuTcwZUZkQZYJiMzqZZWObdDJzmspg66EvM7moZ5NwWF7HZfCr6kaZXeBOjh0QpSoyBvmOq0Emh85KXNZeZUaLg66d6l6w6666n60000KdyR16081R6K8c03e0WOiyooMCBxS0D7MpMAQTMFK4evm4ZIFZLZP0JE1p600jPPPczs03d9C0yhJJZobdjNaHo2hP9KvBFDkZJiZbTZTuLBOQWSTuYR40jcBjzkdcKZOkk7djSt00O7pBt8hXyHWUWFRdWzZ"
-PLACE = "**VV**SVVSS***VV*SSS*VSV*VS*SVSSS*VVVSS*VVS**VVSVV**SVSSSVS**S**VSV*SV*SV**V*VV*"
+ORDER = """
+ccA sc2A ciB sc0A sh1A g11A/S rcp3A zoB- zoA- g13A/S ab2A+ sqB++ zsA ab3A ab0A+ ab2B+ g22B/S g10B/S zcB gzA/S+++ g11B/S hb0A/V hb1A/V sc3A lqB siA kiB okA sc0B sh0A okmA/V puA ulB hb0B/V su0B kp1A sub0B rev3A+ ztA+ sh0B gzB/S+ cnB zsB yzA sc1B ciA ofmA hb2A/V+ ofcA ylB- kbB hb1B/V nbA puB g22A/V g20A/S++ ab1B+ zcA ab3B okmB/S+ ab0B yzB g21A/S sub0A okB siB loA+ g23A/V rvA sub2A rev3B+ cnt0A+ sub1A uB rcp3B+ g21B/S+++ g12A/S+ ab1A nthB cwA sqA++ sub1B wmB uA+ sub3A nokA lastB++ ztB sh1B kp0A su1A+++ nokB ccB hb3A/V+ kbA kwB cwB cmA kiA putA+ g23B/V loB+ kjB g20B/V oflA kwA restA kaA kjA eiB oflB rvB kaB cmB cnt1B+ cut2B ylA ofiA sendA restB sendB yiA ulA+ sub2B sub3B su0A++ lastA+ wmA+ su1B+ kp1B cnt0B+ kp0B cnt1A++ cutB ofmB+ newA+ ofiB eaB yiB newB putB nbB thrB ofcB+ uhB+ sc1A+ lqA+ uhA+ g10A/V+
+"""
+
+
+def places():
+    pos, place = {}, {}
+    names = ORDER.split()
+    for j, w in enumerate(names):
+        lap = w.count("+") - w.count("-")
+        w, _, q = w.strip("+-").partition("/")
+        pos[w] = j - lap * len(names)
+        if q:
+            place[w] = q
+    return pos, place, len(names)
 
 
 def plan():
     if not PLAN:
         ops = build()
         link(ops)
-        both = [op for op in ops if len(op["q"]) > 1]
-        if len(SHIFT) == len(ops) and len(PLACE) == len(both):
-            for op, p in zip(both, PLACE):
-                op["q"] = op["q"] if p == "*" else p
-            seq, total = schedule(ops, 0.0, [(ABC.index(x) - 31) * 0.12 for x in SHIFT])
-        else:
-            seq, total = schedule(ops, 8.0)
-        PLAN["ops"], PLAN["seq"], PLAN["total"] = ops, seq, total
+        pos, place, span = places()
+        for op in ops:
+            op["on"] = place.get(op["name"], op["q"][0])
+        PLAN["ops"] = ops
+        PLAN["seq"] = issue(ops, pos, span)
     return PLAN["ops"], PLAN["seq"]
-
-
-def bits(topo, src, dst):
-    return sum(1 << e for e in topo.engines(src, dst)[:NE])
 
 
 def helper(topo, core, dst):
@@ -451,7 +476,8 @@ def helper(topo, core, dst):
 def send(g, T, topo, core, dst, out, src, rsem):
     rid, pid = topo.addr(dst, core)
     (ob, o0, o1), (ib, i0, i1) = at(out), at(src)
-    g.remote_dma(out_ap=T[ob][:, o0:o1], in_ap=T[ib][:, i0:i1], remote_sem=T.sem[rsem], local_sem=T.sem["lsem"], pid=pid, routing_id=rid, dma_engine_mask=bits(topo, core, dst))
+    g.remote_dma(out_ap=T[ob][:, o0:o1], in_ap=T[ib][:, i0:i1], remote_sem=T.sem[rsem], local_sem=T.sem["lsem"], pid=pid, routing_id=rid, dma_engine_mask=topo.mask(core, dst))
+    return len(topo.engines(core, dst))
 
 
 def rank_program(g, core, T, topo):
@@ -460,11 +486,16 @@ def rank_program(g, core, T, topo):
         for r, c in enumerate(T.cores):
             dst = T.cores[(r + HOPS[1]) % N]
             if not topo.may_write(c, dst) and helper(topo, c, dst) == core:
+                sent = 0
                 for t in range(1, RO):
-                    g.wait_ge(T.sem["h%d" % t], NE)
-                    send(g, T, topo, core, dst, "land%d1" % t, "rel%d" % t, "a%d1" % t)
-                g.wait_ge(T.sem["lsem"], NE * (RO - 1))
+                    g.wait_ge(T.sem["h%d" % t], len(topo.engines(c, core)))
+                    sent += send(g, T, topo, core, dst, "land%d1" % t, "rel%d" % t, "a%d1" % t)
+                g.wait_ge(T.sem["lsem"], sent)
         return
+    arrive = []
+    for hop in HOPS:
+        src = T.cores[(rank - hop) % N]
+        arrive.append(len(topo.engines(src if topo.may_write(src, core) else helper(topo, src, core), core)))
     ops, seq = plan()
     eng = {"V": g.vector, "S": g.scalar, "T": g.tensor, "G": g, "Y": g.sync}
     semn = {"V": "sV", "S": "sS", "T": "sT", "G": "sG"}
@@ -473,16 +504,15 @@ def rank_program(g, core, T, topo):
     g.scalar.dma_start(T.wi[:, :], T.wt[:, :]).then_inc(T.sem["dw"], 16)
     g.scalar.dma_start(T.ki[:, :], T.kn[:, :]).then_inc(T.sem["dk"], 16)
     g.scalar.dma_start(T.li[:, :], T.lim[:, :]).then_inc(T.sem["dl"], 16)
-    count = {q: 0 for q in "VSTG"}
+    count = {}
     known = {q: {} for q in "VSTGY"}
     done, snap = {}, {}
-    sends = 0
-    outs = []
+    sent = 0
     for k in seq:
         op = ops[k]
         q = op["on"]
         if q == "E":
-            done[k] = op["fn"]
+            done[k] = op["fn"] if op["after"] is None else (op["fn"][0], arrive[op["after"][1]])
             snap[k] = {}
             continue
         e = eng[q]
@@ -507,23 +537,16 @@ def rank_program(g, core, T, topo):
             t, b, nb = op["send"]
             dst = T.cores[(rank + HOPS[b]) % N]
             if topo.may_write(core, dst):
-                send(g, T, topo, core, dst, "land%d%d" % (t + 1, b), nb, "a%d%d" % (t + 1, b))
+                sent += send(g, T, topo, core, dst, "land%d%d" % (t + 1, b), nb, "a%d%d" % (t + 1, b))
             else:
-                send(g, T, topo, core, helper(topo, core, dst), "rel%d" % (t + 1), nb, "h%d" % (t + 1))
-            sends += 1
-        elif q == "Y":
-            o, h0, h1, src, sm = op["fn"]
-            e.dma_start(T[o][:, h0:h1], T[src][:, :]).then_inc(T.sem[sm], 16)
-            outs.append(sm)
-        else:
-            ins = op["fn"](e, T, q == "S") if op.get("gat") else op["fn"](e, T)
-            for x in ins:
-                x.then_inc(T.sem[semn[q]], 1)
-            count[q] += len(ins)
-            done[k] = (semn[q], count[q])
-    for sm in outs:
-        g.sync.wait_ge(T.sem[sm], 16)
-    for q in "VSTG":
-        if count[q]:
-            g.sync.wait_ge(T.sem[semn[q]], count[q])
-    g.wait_ge(T.sem["lsem"], NE * sends)
+                sent += send(g, T, topo, core, helper(topo, core, dst), "rel%d" % (t + 1), nb, "h%d" % (t + 1))
+            continue
+        ins = op["fn"](e, T, q == "S") if op.get("both") else op["fn"](e, T)
+        s, n = op.get("sem") or semn[q], 16 if q == "Y" else 1
+        for x in ins:
+            x.then_inc(T.sem[s], n)
+        count[s] = count.get(s, 0) + n * len(ins)
+        done[k] = (s, count[s])
+    for s in sorted(count):
+        g.sync.wait_ge(T.sem[s], count[s])
+    g.wait_ge(T.sem["lsem"], sent)

@@ -4,7 +4,7 @@ N, RO, TU, BL = 8, 4, 256, 128
 HOPS = [4, 1]
 A_ = AluOpType
 F_ = ActivationFunctionType
-OPT = dict(RV=1, TAIL=0, C1=(32, 64))
+OPT = dict(RV=1, TAIL=0, C1=(32, 32), TTU=True)
 COST = dict(f=1.1, gat=1.56, sca=4.0, lat=0.22, vfix=0.04, pe=0.000417, near=2.3, far=3.8, issue=1.0, dma=2.5, load=6.0)
 
 SCRATCH = {}
@@ -37,7 +37,7 @@ for _b in (0, 1):
                        ("uu", 256, "int32"), ("ofm", 24, "uint16"), ("zt", 128, "bfloat16"), ("zz", 128, "float32"),
                        ("ci", 128, "int32"), ("cc", 128, "int32"), ("ofc", 128, "uint16"), ("ofi", 8, "uint16"),
                        ("rv", 128, "float32"), ("cm", 128, "float32"), ("out", 128, "float32"), ("zo", 128, "float32"),
-                       ("yi", 128, "int32"), ("kw", 128, "float32"), ("ka", 8, "int32"), ("kb", 8, "int32"),
+                       ("yi", 128, "int32"), ("kw", 128, "int32"), ("ka", 8, "int32"), ("kb", 8, "int32"),
                        ("kc", 8, "int32"), ("kd", 8, "int32"), ("ofl", 8, "uint16"), ("cw", 2048, "int32")):
         buf(_n + str(_b), _c, _d)
 for _n, _c, _d in (("cn", 1, "bfloat16"), ("ei", 1, "int32"), ("ea", 1, "int32"), ("thr", 4, "float32"), ("nth", 4, "float32"),
@@ -248,7 +248,7 @@ def build():
             for h in (0, 1):
                 c0, c1 = o + 1024 * h, o + 1024 * h + 1024
                 TE("su%d" % h, 1024, mms([(P(QB, 64 * h, 64 * h + 64), blk("wr", i), P("gg", c0 + i, c1, 16)) for i in range(16)]), ["wr", ("gg", c0, c1)], [(QB, 64 * h, 64 * h + 64)])
-                TE("cnt%d" % h, 1024, mms([(P(QA, 64 * h, 64 * h + 64), blk("ind", i), P("hb", c0 + i, c1, 16)) for i in range(16)]), ["ind", ("hb", c0, c1)], [(QA, 64 * h, 64 * h + 64)])
+                TE("cnt%d" % h, 960, mms([(P(QA, 64 * h, 64 * h + 64), blk("ind", i), P("hb", c0 + i, c1, 16)) for i in range(1, 16)]), ["ind", ("hb", c0, c1)], [(QA, 64 * h, 64 * h + 64)])
             V("si", 128, tc(B("si"), P(QB, 0, 128)), [(QB, 0, 128)], ["si" + sb])
             V("ul", 128, ts(B("uu", 0, 128), B("si"), 15, None, A_.bitwise_and), ["si" + sb], [("uu" + sb, 0, 128)])
             V("uh", 128, ts(B("uu", 128, 256), B("si"), 4080, None, A_.bitwise_and), ["si" + sb], [("uu" + sb, 128, 256)])
@@ -297,17 +297,22 @@ def build():
                         items = [(P(QB, 0, 128), row("ones", 2, 0, 128), row("krow", 2, 0, 128))] + items
                     TE("kp%d" % h, 1024 + 128 * (h == 0), mms(items, h == 0, h == 1), ["ones", "krow", "ind", ("aa", c1 - 1024, c1)], [(QB, 0, 128)])
             V("kw", 128, scan(B("kw"), P("rs2"), P(QB, 0, 128)), ["rs2", (QB, 0, 128)], ["kw" + sb])
-            V("ka", 8, tc(B("ka"), B("kw", 15, 128, 16)), ["kw" + sb], ["ka" + sb])
-            V("kb", 8, ts(B("kb"), B("ka"), 2047, None, A_.bitwise_and), ["ka" + sb], ["kb" + sb])
+            least = B("kw", 15, 128, 16)
+            V("kb", 8, ts(B("kb"), least, 2047, None, A_.bitwise_and), ["kw" + sb], ["kb" + sb])
             V("ofl", 8, ts(B("ofl"), B("kb"), col(0), None, A_.add), ["kb" + sb, c(0)], ["ofl" + sb])
-            VG("new", 128, tt(B("out"), by(("cw" + sb,), ("ofl" + sb,)), B("cm"), A_.add), ["cw" + sb, "ofl" + sb, "cm" + sb], ["out" + sb])
+            nb = "out" + sb if last or not OPT["TTU"] else "nb%d%d" % (t + 1, b)
+            VG("new", 128, tt(P(nb), by(("cw" + sb,), ("ofl" + sb,)), B("cm"), A_.add), ["cw" + sb, "ofl" + sb, "cm" + sb], [nb])
             if not last:
-                nb = "nb%d%d" % (t + 1, b)
-                V("nb", 128, tc(P(nb), B("out")), ["out" + sb], [nb])
+                if not OPT["TTU"]:
+                    nb = "nb%d%d" % (t + 1, b)
+                    V("nb", 128, tc(P(nb), B("out")), ["out" + sb], [nb])
                 add("send", "G", {"G": ("i", 0)}, None, [nb], [], send=(t, b, nb))
-                V("ki", 8, ts(B("kc"), B("ka"), 7, 15, A_.arith_shift_right, A_.bitwise_and), ["ka" + sb], ["kc" + sb])
-                V("kj", 8, tt(B("kd"), B("kc"), P("cv", 0, 8), A_.add), ["kc" + sb, ("cv", 0, 8)], ["kd" + sb])
-                V("ofi", 8, tc(B("ofi"), B("kd")), ["kd" + sb], ["ofi" + sb])
+                V("ki", 8, ts(B("kc"), least, 7, 15, A_.arith_shift_right, A_.bitwise_and), ["kw" + sb], ["kc" + sb])
+                if OPT["TTU"]:
+                    V("ofi", 8, tt(B("ofi"), B("kc"), P("cv", 0, 8), A_.add), ["kc" + sb, ("cv", 0, 8)], ["ofi" + sb])
+                else:
+                    V("kj", 8, tt(B("kd"), B("kc"), P("cv", 0, 8), A_.add), ["kc" + sb, ("cv", 0, 8)], ["kd" + sb])
+                    V("ofi", 8, tc(B("ofi"), B("kd")), ["kd" + sb], ["ofi" + sb])
                 VG("yi", 128, tt(B("yi"), by(("hh", o, o + 2048), ("ofi" + sb,)), B("zz"), A_.add), [("hh", o, o + 2048), "ofi" + sb, "zz" + sb], ["yi" + sb])
             else:
                 S("zo", 128, act(B("zo"), B("zz"), F_.Identity, 0.5, 2.0), ["zz" + sb], ["zo" + sb])
@@ -438,31 +443,44 @@ def issue(ops, pos, span):
 
 PLAN = {}
 ORDER = """
-ccA sc2A ciB sc0A sh1A g11A/S rcp3A zoB- zoA- g13A/S ab2A+ sqB++ zsA ab3A ab0A+ ab2B+ g22B/S g10B/S zcB gzA/S+++ g11B/S hb0A/V hb1A/V sc3A lqB siA kiB okA sc0B sh0A okmA/V puA ulB hb0B/V su0B kp1A sub0B rev3A+ ztA+ sh0B gzB/S+ cnB zsB yzA sc1B ciA ofmA hb2A/V+ ofcA ylB- kbB hb1B/V nbA puB g22A/V g20A/S++ ab1B+ zcA ab3B okmB/S+ ab0B yzB g21A/S sub0A okB siB loA+ g23A/V rvA sub2A rev3B+ cnt0A+ sub1A uB rcp3B+ g21B/S+++ g12A/S+ ab1A nthB cwA sqA++ sub1B wmB uA+ sub3A nokA lastB++ ztB sh1B kp0A su1A+++ nokB ccB hb3A/V+ kbA kwB cwB cmA kiA putA+ g23B/V loB+ kjB g20B/V oflA kwA restA kaA kjA eiB oflB rvB kaB cmB cnt1B+ cut2B ylA ofiA sendA restB sendB yiA ulA+ sub2B sub3B su0A++ lastA+ wmA+ su1B+ kp1B cnt0B+ kp0B cnt1A++ cutB ofmB+ newA+ ofiB eaB yiB newB putB nbB thrB ofcB+ uhB+ sc1A+ lqA+ uhA+ g10A/V+
+V: eiB- kiB- kbB- eaB- ofiB- oflB- yiB- newB- putB- thrB- lqA g10A g13A sc1A sc0A sc2A sc3A hb0A lqB hb1A hb3A hb2A siA sc3B uhA sc0B ulA okA hb3B sc1B puA okmA hb1B hb0B sc2B ciA ofmA ccA gzA ofcA hb2B g20A siB okB uhB ulB okmB puB g22A cmA ciB ofmB ccB gzB ofcB g21B g20B kwA rvA kbA restA oflA newA kiA cmB rvB ofiA restB loA+ loB+ yiA putA kwB
+S: rcp3A g13B g10B g11B rcp3B g12B zsA sqA zsB zcA g23A g21A ab0A sqB ab3A ab1A ab2A zcB g23B zoB- g22B ab1B zoA- ab0B ab3B ab2B cnB g11A+ nthB g12A+
+T: sub3A- uB- wmB- sub1A- sub2A- ztB- kp0A- kp1A- sub1B- sub0B- sub3B- nokB- sub2B- kp0B- cutB- kp1B- cut2B- rev3A su0A su1A rev3B cnt0A cnt1A lastA su0B uA wmA cnt0B su1B ztA cnt1B sub0A lastB nokA
+G: sendA sendB
+Y: yzB yzA- ylA sh0A+ sh0B+ sh1A+ cwA+ ylB- sh1B+ cwB+
 """
 
 
-def places():
-    pos, place = {}, {}
-    names = ORDER.split()
-    for j, w in enumerate(names):
-        lap = w.count("+") - w.count("-")
-        w, _, q = w.strip("+-").partition("/")
-        pos[w] = j - lap * len(names)
-        if q:
-            place[w] = q
-    return pos, place, len(names)
+def issue(ops):
+    which = {(op["name"], op["t"]): k for k, op in enumerate(ops)}
+    before = [set(op["deps"] | op["order"]) for op in ops]
+    for op in ops:
+        op["on"] = op["q"]
+    for line in ORDER.strip().split("\n"):
+        q, names = line.split(":")
+        row = [k for k, op in enumerate(ops) if op["t"] < 0 and op["q"] == q]
+        for t in range(-1, RO + 1):
+            for w in names.split():
+                k = which.get((w.strip("+-"), t + w.count("+") - w.count("-")))
+                if k is not None and ops[k]["t"] >= 0:
+                    row.append(k)
+        for j, k in enumerate(row):
+            ops[k]["on"] = q
+            before[k].update(row[j - 1:j])
+    seq, seen = [], set()
+    while len(seq) < len(ops):
+        go = [k for k in range(len(ops)) if k not in seen and before[k] <= seen]
+        assert go
+        seq += go
+        seen.update(go)
+    return seq
 
 
 def plan():
     if not PLAN:
         ops = build()
         link(ops)
-        pos, place, span = places()
-        for op in ops:
-            op["on"] = place.get(op["name"], op["q"][0])
-        PLAN["ops"] = ops
-        PLAN["seq"] = issue(ops, pos, span)
+        PLAN["ops"], PLAN["seq"] = ops, issue(ops)
     return PLAN["ops"], PLAN["seq"]
 
 

from concourse.mybir import dt, AluOpType, ActivationFunctionType

N, RO, TU, BL = 8, 4, 256, 128
HOPS = [4, 1]
A_ = AluOpType
F_ = ActivationFunctionType
OPT = dict(RV=1, TAIL=0, C1=(32, 32), TTU=True)
COST = dict(f=1.1, gat=1.56, sca=4.0, lat=0.22, vfix=0.04, pe=0.000417, near=2.3, far=3.8, issue=1.0, dma=2.5, load=6.0)

SCRATCH = {}


def buf(name, cols, dtype, where="sbuf"):
    SCRATCH[name] = (where, [128] + (cols if isinstance(cols, list) else [cols]), dtype)


for _n in ("xs", "gg", "mm", "hb", "hh"):
    buf(_n, 4096, "bfloat16")
buf("aa", [16, 16, 16], "bfloat16")
buf("l0", 256, "int32"); buf("lo0", 256, "uint16")
buf("rel", BL * 3, "uint16"); buf("land", BL * 6, "uint16"); buf("nb", BL * 6, "uint16")
PART = {}
for _t in range(1, RO):
    PART["rel%d" % _t] = ("rel", BL * (_t - 1))
    for _b in (0, 1):
        PART["land%d%d" % (_t, _b)] = ("land", BL * (2 * _t - 2 + _b))
        PART["nb%d%d" % (_t, _b)] = ("nb", BL * (2 * _t - 2 + _b))


def at(name, a=0, b=BL):
    n, o = PART[name]
    return n, o + a, o + b


for _b in (0, 1):
    for _n, _c, _d in (("lq", 128, "float32"), ("sk", 2048, "float32"), ("ok", 512, "bfloat16"), ("si", 128, "int32"),
                       ("uu", 256, "int32"), ("ofm", 24, "uint16"), ("zt", 128, "bfloat16"), ("zz", 128, "float32"),
                       ("ci", 128, "int32"), ("cc", 128, "int32"), ("ofc", 128, "uint16"), ("ofi", 8, "uint16"),
                       ("rv", 128, "float32"), ("cm", 128, "float32"), ("out", 128, "float32"), ("zo", 128, "float32"),
                       ("yi", 128, "int32"), ("kw", 128, "int32"), ("ka", 8, "int32"), ("kb", 8, "int32"),
                       ("kc", 8, "int32"), ("kd", 8, "int32"), ("ofl", 8, "uint16"), ("cw", 2048, "int32")):
        buf(_n + str(_b), _c, _d)
for _n, _c, _d in (("cn", 1, "bfloat16"), ("ei", 1, "int32"), ("ea", 1, "int32"), ("thr", 4, "float32"), ("nth", 4, "float32"),
                   ("wi", 1, "int32"), ("ki", 1, "int32"), ("li", 4, "int32"),
                   ("pc", 1, "int32"), ("pi", 1, "int32"), ("cols", 16, "float32"), ("gs", 8, "float32"), ("gw", 8, "float32"),
                   ("bo", 128, "bfloat16"), ("idb", 128, "bfloat16"), ("nid", 128, "bfloat16"),
                   ("nif", 128, "float32"), ("dm", 128, "bfloat16"), ("up", 128, "bfloat16"),
                   ("ind", 2048, "bfloat16"), ("wr", 2048, "bfloat16"), ("sh", 512, "float32"), ("ex", 2048, "bfloat16"),
                   ("ones", 2048, "bfloat16"), ("rst", 1024, "bfloat16"), ("rs2", 128, "float32"),
                   ("cr", 16, "float32"), ("cv", 48, "bfloat16"), ("s15", 1, "bfloat16"),
                   ("krow", 128, "bfloat16"), ("bm", 128, "float32")):
    buf(_n, _c, _d)
for _n in range(8):
    buf("q%d" % _n, 512, "float32", "psum")

SEMAPHORES = ["sV", "sS", "sT", "sG", "dx", "dt", "dw", "dk", "dl", "lsem", "o00", "o01", "o10", "o11", "r00", "r01", "r10", "r11", "w0", "w1"]
SEMAPHORES += ["a%d%d" % (_t, _b) for _t in range(1, RO) for _b in (0, 1)] + ["h%d" % _t for _t in range(1, RO)]


def width(name):
    n = 1
    for x in SCRATCH[name][1][1:]:
        n *= x
    return n


def build():
    ops = []
    now = {"t": -1, "b": ""}
    TAIL, RV = OPT["TAIL"], OPT["RV"]

    def R(x):
        return [y if isinstance(y, tuple) else at(y) if y in PART else (y, 0, width(y)) for y in x]

    def add(name, q, cost, fn, rd, wr, **more):
        ops.append(dict(name=name + now["b"], t=now["t"], q=q, c=cost, fn=fn, rd=R(rd), wr=R(wr), **more))

    def V(name, cyc, fn, rd, wr):
        add(name, "V", {"V": ("v", cyc)}, lambda e, T: [fn(e, T)], rd, wr)

    def VG(name, n, fn, rd, wr, kind="gv"):
        add(name, "V", {"V": (kind, n)}, lambda e, T: [fn(e, T)], rd, wr)

    def S(name, cyc, fn, rd, wr):
        add(name, "S", {"S": ("s", cyc)}, lambda e, T: [fn(e, T)], rd, wr)

    def VS(name, cv, cs, fv, fs, rd, wr, kinds="vs"):
        add(name, "VS", {"V": (kinds[0], cv), "S": (kinds[1], cs)}, lambda e, T, scalar: [(fs if scalar else fv)(e, T)], rd, wr, both=True)

    def TE(name, cyc, fn, rd, wr):
        add(name, "T", {"T": ("t", cyc)}, fn, rd, wr)

    def GP(cyc, fn, rd, wr):
        add("c", "G", {"G": ("g", cyc)}, lambda e, T: [fn(e, T)], rd, wr)

    def C(cyc, fn, rd, wr):
        V("c", cyc, fn, rd, wr)

    def ev(sem, val, b, late, after=None):
        add("ev", "E", {"E": ("0", 0)}, (sem, val), [], [b], late=late, after=after)

    def num(x):
        return isinstance(x, (int, float)) or x is None

    def val(x, T):
        return x if num(x) else x(T)

    def ts(out, in0, s1, s2, *op):
        return lambda e, T: e.tensor_scalar(out(T), in0(T), val(s1, T), val(s2, T), *op)

    def tt(out, a, b, op):
        return lambda e, T: e.tensor_tensor(out(T), a(T), b(T), op)

    def tc(out, a):
        return lambda e, T: e.tensor_copy(out(T), a(T))

    def act(out, a, func, bias=0.0, scale=1.0):
        return lambda e, T: e.activation(out(T), a(T), func, bias=val(bias, T), scale=val(scale, T))

    def scan(out, d0, d1):
        return lambda e, T: e.tensor_tensor_scan(out(T), d0(T), d1(T), 0.0, A_.add, A_.min)

    def P(name, a=None, b=None, step=None):
        if name in PART:
            name, a, b = at(name) if a is None else at(name, a, b)
        return (lambda T: T[name][:, :]) if a is None else (lambda T: T[name][:, a:b:step]) if step else (lambda T: T[name][:, a:b])

    def by(win, off):
        return lambda T: P(*win)(T).indirect(P(*off)(T))

    def gat(name, dst, win, off, scale=1.0, bias=0.0):
        n = dst[2] - dst[1]
        fv = tc(P(*dst), by(win, off)) if scale == 1.0 else ts(P(*dst), by(win, off), scale, bias, A_.mult, A_.add)
        VS(name, n, n, fv, act(P(*dst), by(win, off), F_.Identity if bias else F_.Copy, bias, scale), [win, off], [dst], ("gv", "gs"))

    def col(j):
        return P("cols", j, j + 1)

    def c(j):
        return ("cols", j, j + 1)

    def mms(items, first=True, last=True):
        return lambda e, T: [e.matmul(o(T), l(T), r(T), first and k == 0, last and k == len(items) - 1) for k, (o, l, r) in enumerate(items)]

    def row(name, k, a, b):
        return lambda T: T[name][0:k, a:b]

    def blk(name, i):
        return P(name, 128 * i, 128 * i + 128)

    XS = ("xs", 0, 4096)
    ev("dx", 16, "xs", "load"); ev("dt", 16, "l0", 3.0); ev("dw", 16, "wi", 2.5); ev("dk", 16, "ki", 2.5); ev("dl", 16, "li", 2.5)
    GP(2, lambda e, T: e.iota(T.pc[:, :], [[0, 1]], 0, 1), [], ["pc"])
    def select(out, src, pattern, op, base, mul, n=128):
        GP(2 * n, lambda e, T: e.affine_select(P(*out)(T), P(*src)(T), pattern, op, 0.0, base, mul), [src], [out])

    def fillc(name, cyc, v, step=None):
        C(cyc, lambda e, T: e.memset(T[name][:, 0::step] if step else T[name][:, :], v), [], [name])

    def spots(name, k):
        add("c", "S", {"S": ("s", 700)}, lambda e, T: [e.activation(T[name][:, 16 * j:min(16 * j + 129 * 16, 2048):129], T.ones[:, 0:16], F_.Copy, scale=T[k][:, j:j + 1]) for j in range(8)], ["ones", k], [name])

    GP(32, lambda e, T: e.iota(T.cr[:, :], [[1, 16]], 0, 0, allow_small_or_imprecise_dtypes=True), [], ["cr"])
    GP(256, lambda e, T: e.iota(T.krow[:, :], [[0, 8], [128, 16]], 0, 0, allow_small_or_imprecise_dtypes=True), [], ["krow"])
    GP(256, lambda e, T: e.iota(T.krow[0:1, :], [[16, 8], [0, 16]], 0, 0, allow_small_or_imprecise_dtypes=True), [], ["krow"])
    fillc("ones", 1024, 1.0)
    fillc("ind", 1024, 0.0)
    O, G16 = ("ones", 0, 128), [[-16, 8], [0, 16]]
    select(("up", 0, 128), O, G16, A_.is_ge, 0, 1)
    select(("bo", 0, 128), ("up", 0, 128), [[16, 8], [0, 16]], A_.is_ge, 15, -1)
    select(("idb", 0, 128), O, [[-1, 128]], A_.is_equal, 0, 1)
    C(1, ts(P("pi"), P("pc"), 15, None, A_.bitwise_and), ["pc"], ["pi"])
    fillc("wr", 1024, 0.0)
    C(1, tc(col(0), P("pi")), ["pi"], [c(0)])
    C(1, ts(col(2), P("pi"), 1.0, None, A_.is_ge), ["pi"], [c(2)])
    C(1, ts(P("s15"), P("pi"), 15.0, None, A_.is_ge), ["pi"], ["s15"])
    fillc("rst", 512, 0.0)
    C(1, tc(col(7), P("wi")), ["wi"], [c(7)])
    C(1, tc(col(10), P("ki")), ["ki"], [c(10)])
    C(1, tc(P("thr", 0, 1), P("li", 0, 1)), ["li"], [("thr", 0, 1)])
    fillc("rst", 64, 1024.0, 16)
    C(1, ts(col(9), P("ki"), col(10), -64.0, A_.mult, A_.mult), ["ki", c(10)], [c(9)])
    fillc("rs2", 128, 0.0)
    S("c", 8, act(P("gs"), P("bo", 0, 128, 16), F_.Copy), ["bo"], ["gs"])
    S("c", 128, act(P("bm"), P("bo"), F_.Copy, 0.0, 1.0 / 2048), ["bo"], ["bm"])
    spots("ind", "gs")
    S("c", 1, act(col(3), col(2), F_.Copy, 0.0, 128.0), [c(2)], [c(3)])
    S("c", 1, act(col(4), col(2), F_.Identity, -20.0, 20.75), [c(2)], [c(4)])
    S("c", 1, act(col(5), col(0), F_.Copy, 0.0, 16.0), [c(0)], [c(5)])
    S("c", 8, act(P("gw"), P("gs"), F_.Copy, 0.0, col(7)), ["gs", c(7)], ["gw"])
    S("c", 1, act(col(8), col(10), F_.Copy, 0.0, 8.0), [c(10)], [c(8)])
    S("c", 1, act(P("nth", 0, 1), P("thr", 0, 1), F_.Identity, 0.5, -1.0), [("thr", 0, 1)], [("nth", 0, 1)])
    spots("wr", "gw")
    for k in range(4 - RV, 4):
        select(("sh", 128 * k, 128 * k + 128), ("bm", 0, 128), [[-16, 8], [1, 16]], A_.is_equal, -(13 + k), 1)
        TE("c", 256, mms([(P("q7", k, k + 1), blk("sh", k), col(9))]), [("sh", 128 * k, 128 * k + 128), c(9)], [("q7", k, k + 1)])
    select(("up", 0, 128), ("bo", 0, 128), [[-1, 128]], A_.is_equal, -1, 1)
    S("c", 128, act(P("nid"), P("idb"), F_.Copy, 0.0, -1.0), ["idb"], ["nid"])
    S("c", 128, act(P("nif"), P("idb"), F_.Copy, 0.0, -1.0), ["idb"], ["nif"])
    for b in (0, 1):
        for j, (a0, mul, k) in enumerate(((0, 256.0, 5), (0, 16.0, 0), (8 * b, 256.0, 5))):
            w = ("cv", 24 * b + 8 * j, 24 * b + 8 * j + 8)
            S("c", 8, act(P(*w), P("cr", a0, a0 + 8), F_.Identity, col(k), mul), ["cr", c(k)], [w])
    for k in range(4 - RV, 4):
        S("c", 1, act(col(12 + k), P("q7", k, k + 1), F_.Copy, 0.0, -1.0), [("q7", k, k + 1)], [c(12 + k)])
    fillc("rs2", 64, 16777216.0, 16)
    C(256, tt(P("dm"), P("idb"), P("up"), A_.subtract), ["idb", "up"], ["dm"])
    for b in (1 - TAIL, TAIL):
        GP(4096, lambda e, T, b=b: e.iota(T["cw%d" % b][:, :], [[0, 2048]], 0, 0), [], ["cw%d" % b])
        if b != TAIL:
            select(("ex", 0, 2048), ("ones", 0, 2048), [[-1, 128], [0, 16]], A_.is_equal, 0, 1, 2048)

    for t in range(RO):
        last = t == RO - 1
        for b in (1 - TAIL, TAIL):
            now["t"], now["b"] = t, "AB"[b == TAIL]
            sb = str(b)
            QA, QB = "q%d" % (2 * b), "q%d" % (2 * b + 1)
            o = 2048 * b
            B = lambda n, *a, sb=sb: P(n + sb, *a)
            if t == 0:
                ob = ("lo0", 128 * b, 128 * b + 128)
                src = ("l0", 128 * b, 128 * b + 128)
                V("lo", 128, tc(P(*ob), P(*src)), [src], [ob])
                S("zs", 1920, lambda e, T, sb=sb: e.activation(T["sk" + sb][96:128, 0:1920], T.ones[96:128, 0:1920], F_.Copy), ["ones"], [("sk" + sb, 0, 1920)])
            else:
                ln = "land%d%d" % (t, b)
                ev("a%d%d" % (t, b), 8, ln, "far" if b else "near", (t - 1, b))
                src = ob = at(ln)
            V("lq", 128, ts(B("lq"), P(*src), 16.0, col(9), A_.mult, A_.add), [src, c(9)], ["lq" + sb])
            for k in range(4 - RV, 4):
                TE("rev%d" % k, 512, mms([(blk(QB, k), blk("sh", k), B("lq"))]), [("sh", 128 * k, 128 * k + 128), "lq" + sb], [(QB, 128 * k, 128 * k + 128)])
            for k in range(4 - RV, 4):
                S("rcp%d" % k, 128, act(blk("sk" + sb, 12 + k), blk(QB, k), F_.Identity, col(12 + k)), [(QB, 128 * k, 128 * k + 128), c(12 + k)], [("sk" + sb, 128 * (12 + k), 128 * (13 + k))])
            for lv, (w, y0) in enumerate(((1, 15), (4, 12))):
                if w >= RV:
                    add("sh%d" % lv, "Y", {"Y": ("y", 3)},
                        lambda e, T, w=w, y0=y0, sb=sb: [e.dma_start(T["sk" + sb][0:128 - s, 128 * (y0 - s):128 * (y0 - s + w)], T["sk" + sb][s:128, 128 * y0:128 * (y0 + w)]) for s in (w, 2 * w, 3 * w)],
                        [("sk" + sb, 128 * y0, 128 * (y0 + w))], [("sk" + sb, 128 * (y0 - 3 * w), 128 * y0)], late="dma", sem="r%d%d" % (lv, b))
            CH = OPT["C1"][b == TAIL]
            for v0 in range(0, 128, CH):
                c0, c1 = o + 16 * v0, o + 16 * (v0 + CH)
                k = str(v0 // CH)
                gat("g1" + k, ("gg", c0, c1), XS, (ob[0], ob[1] + v0, ob[1] + v0 + CH))
                V("sc" + k, 8 * CH, scan(P("mm", c0, c1), P("rst", 0, c1 - c0), P("gg", c0, c1)), ["rst", ("gg", c0, c1)], [("mm", c0, c1)])
                VS("hb" + k, 8 * CH, 16 * CH, ts(P("hb", c0, c1), P("mm", c0, c1), P("thr", t, t + 1), 0.5, A_.is_ge, A_.subtract),
                   act(P("hb", c0, c1), P("mm", c0, c1), F_.Sign, P("nth", t, t + 1)), [("mm", c0, c1), ("thr", t, t + 1), ("nth", t, t + 1)], [("hb", c0, c1)])
            for h in (0, 1):
                c0, c1 = o + 1024 * h, o + 1024 * h + 1024
                TE("su%d" % h, 1024, mms([(P(QB, 64 * h, 64 * h + 64), blk("wr", i), P("gg", c0 + i, c1, 16)) for i in range(16)]), ["wr", ("gg", c0, c1)], [(QB, 64 * h, 64 * h + 64)])
                TE("cnt%d" % h, 960, mms([(P(QA, 64 * h, 64 * h + 64), blk("ind", i), P("hb", c0 + i, c1, 16)) for i in range(1, 16)]), ["ind", ("hb", c0, c1)], [(QA, 64 * h, 64 * h + 64)])
            V("si", 128, tc(B("si"), P(QB, 0, 128)), [(QB, 0, 128)], ["si" + sb])
            V("ul", 128, ts(B("uu", 0, 128), B("si"), 15, None, A_.bitwise_and), ["si" + sb], [("uu" + sb, 0, 128)])
            V("uh", 128, ts(B("uu", 128, 256), B("si"), 4080, None, A_.bitwise_and), ["si" + sb], [("uu" + sb, 128, 256)])
            ok, okm, pl = (("ok" + sb, 128 * j, 128 * j + 128) for j in range(3))
            V("ok", 128, ts(P(*ok), P(QA, 0, 128), col(4), None, A_.is_ge), [(QA, 0, 128), c(4)], [ok])
            TE("last", 256, lambda e, T, QA=QA, ok=ok: [e.matmul(T[QA][:, a:a + 128], T.dm[:, :], P(*ok)(T), True, True) for a in (128, 256)], ["dm", ok], [(QA, 128, 384)])
            V("pu", 256, tt(B("ok", 256, 512), B("uu"), P(QA, 128, 384), A_.mult), ["uu" + sb, (QA, 128, 384)], [("ok" + sb, 256, 512)])
            TE("u", 256, mms([(P(QB, 128, 256), P("bo"), B("ok", a, a + 128)) for a in (256, 384)]), ["bo", ("ok" + sb, 256, 512)], [(QB, 128, 256)])
            VS("okm", 64, 128, ts(P(*okm), P(*ok), col(3), None, A_.mult), act(P(*okm), P(*ok), F_.Copy, 0.0, col(3)), [ok, c(3)], [okm])
            nw = 16 if last else 24
            W = P(QA, 384, 384 + nw)
            TE("wm", 18 * 64, mms([(W, P("idb"), P("cv", 24 * b, 24 * b + nw)), (P(QA, 384, 392), P("nid"), P("ones", 0, 8))] +
                                  [(W, blk("ind", r), B("ok", r, 16 * nw, 16)) for r in range(16)]),
               ["idb", "cv", "ones", "nid", "ind", ("ok" + sb, 0, 16 * nw)], [(QA, 384, 384 + nw)])
            V("ofm", 24, tc(B("ofm", 0, nw), W), [(QA, 384, 384 + nw)], ["ofm" + sb])
            S("sq", 128, act(P(QB, 256, 384), P(QB, 128, 256), F_.Square, col(8)), [(QB, 128, 256), c(8)], [(QB, 256, 384)])
            V("ci", 128, tt(B("ci"), B("lq"), P(QB, 256, 384), A_.add), ["lq" + sb, (QB, 256, 384)], ["ci" + sb])
            V("cc", 128, ts(B("cc"), B("ci"), 4, 4095, A_.arith_shift_right, A_.bitwise_and), ["ci" + sb], ["cc" + sb])
            V("ofc", 128, tc(B("ofc"), B("cc")), ["cc" + sb], ["ofc" + sb])
            add("cw", "Y", {"Y": ("y", 1)}, lambda e, T, sb=sb: [e.dma_start(T["cw" + sb][0:128:16, :], T["cc" + sb][:, :])], ["cc" + sb], ["cw" + sb], late="dma", sem="w" + sb)
            gat("gz", ("zz" + sb, 0, 128), ("mm", o, o + 2048), ("ofm" + sb, 0, 8), 0.5, -0.25)
            TE("zt", 512, mms([(P(QA, 0, 128), B("zz"), P("nif"))]), ["zz" + sb, "nif"], [(QA, 0, 128)])
            S("zc", 128, act(B("zt"), P(QA, 0, 128), F_.Identity, -0.25), [(QA, 0, 128)], ["zt" + sb])
            TE("nok", 256, mms([(P(QA, 128, 256), P("nid"), P(*ok)), (P(QA, 128, 256), row("ones", 1, 0, 128), row("ones", 1, 0, 128))]), ["nid", ok, "ones"], [(QA, 128, 256)])
            VG("rv", 128, tt(B("rv"), by(("sk" + sb,), ("ofm" + sb, 8, 16)), P(*okm), A_.mult), ["sk" + sb, ("ofm" + sb, 8, 16), okm], ["rv" + sb])
            V("cm", 128, tt(P(QA, 256, 384), B("cc"), P(QA, 128, 256), A_.mult), ["cc" + sb, (QA, 128, 256)], [(QA, 256, 384)])
            V("rest", 128, tt(B("cm"), B("rv"), P(QA, 256, 384), A_.add), ["rv" + sb, (QA, 256, 384)], ["cm" + sb])
            if b == TAIL and not last:
                TE("cut", 128, mms([(P(QA, 408, 409), P("ok%d" % j, 0, 128), P("s15")) for j in (0, 1)]), [("ok0", 0, 128), ("ok1", 0, 128), "s15"], [(QA, 408, 409)])
                S("cn", 1, act(P("cn"), P(QA, 408, 409), F_.Copy), [(QA, 408, 409)], ["cn"])
                TE("cut2", 64, mms([(P(QA, 409, 410), P("ones", 0, 128), P("cn"))]), ["ones", "cn"], [(QA, 409, 410)])
                V("ei", 1, ts(P("ei"), P(QA, 409, 410), -1.0, 2048.0, A_.mult, A_.add), [(QA, 409, 410)], ["ei"])
                V("ea", 1, ts(P("ea"), P("ei"), 7, None, A_.bitwise_and), ["ei"], ["ea"])
                V("thr", 1, tt(P("thr", t + 1, t + 2), P("li", t + 1, t + 2), P("ea"), A_.add), ["li", "ea"], [("thr", t + 1, t + 2)])
                S("nth", 1, act(P("nth", t + 1, t + 2), P("thr", t + 1, t + 2), F_.Identity, 0.5, -1.0), [("thr", t + 1, t + 2)], [("nth", t + 1, t + 2)])
            for k in range(4):
                Q = "q%d" % (4 + k)
                c0, c1 = o + 512 * k, o + 512 * k + 512
                gat("g2%d" % k, ("hh", c0, c1), XS, ("ofc" + sb, 32 * k, 32 * k + 32), 0.5)
                TE("sub%d" % k, 1024, mms([(P(Q), B("zt"), P("ex", 512 * k, 512 * k + 512)), (P(Q), P("idb"), P("hh", c0, c1))]), ["zt" + sb, "ex", "idb", ("hh", c0, c1)], [Q])
                S("ab%d" % k, 512, act(lambda T, c0=c0, c1=c1: T.aa[:, c0 // 256:c1 // 256, :, :], P(Q), F_.Abs, 0.0, 4096.0), [Q], [("aa", c0, c1)])
                if k % 2:
                    h = k // 2
                    items = [(P(QB, 64 * h, 64 * h + 64), blk("ind", r), lambda T, r=r, a=8 * b + 4 * h: T.aa[:, a:a + 4, r, :]) for r in range(16)]
                    if h == 0:
                        items = [(P(QB, 0, 128), row("ones", 2, 0, 128), row("krow", 2, 0, 128))] + items
                    TE("kp%d" % h, 1024 + 128 * (h == 0), mms(items, h == 0, h == 1), ["ones", "krow", "ind", ("aa", c1 - 1024, c1)], [(QB, 0, 128)])
            V("kw", 128, scan(B("kw"), P("rs2"), P(QB, 0, 128)), ["rs2", (QB, 0, 128)], ["kw" + sb])
            least = B("kw", 15, 128, 16)
            V("kb", 8, ts(B("kb"), least, 2047, None, A_.bitwise_and), ["kw" + sb], ["kb" + sb])
            V("ofl", 8, ts(B("ofl"), B("kb"), col(0), None, A_.add), ["kb" + sb, c(0)], ["ofl" + sb])
            nb = "out" + sb if last or not OPT["TTU"] else "nb%d%d" % (t + 1, b)
            VG("new", 128, tt(P(nb), by(("cw" + sb,), ("ofl" + sb,)), B("cm"), A_.add), ["cw" + sb, "ofl" + sb, "cm" + sb], [nb])
            if not last:
                if not OPT["TTU"]:
                    nb = "nb%d%d" % (t + 1, b)
                    V("nb", 128, tc(P(nb), B("out")), ["out" + sb], [nb])
                add("send", "G", {"G": ("i", 0)}, None, [nb], [], send=(t, b, nb))
                V("ki", 8, ts(B("kc"), least, 7, 15, A_.arith_shift_right, A_.bitwise_and), ["kw" + sb], ["kc" + sb])
                if OPT["TTU"]:
                    V("ofi", 8, tt(B("ofi"), B("kc"), P("cv", 0, 8), A_.add), ["kc" + sb, ("cv", 0, 8)], ["ofi" + sb])
                else:
                    V("kj", 8, tt(B("kd"), B("kc"), P("cv", 0, 8), A_.add), ["kc" + sb, ("cv", 0, 8)], ["kd" + sb])
                    V("ofi", 8, tc(B("ofi"), B("kd")), ["kd" + sb], ["ofi" + sb])
                VG("yi", 128, tt(B("yi"), by(("hh", o, o + 2048), ("ofi" + sb,)), B("zz"), A_.add), [("hh", o, o + 2048), "ofi" + sb, "zz" + sb], ["yi" + sb])
            else:
                S("zo", 128, act(B("zo"), B("zz"), F_.Identity, 0.5, 2.0), ["zz" + sb], ["zo" + sb])
                for k, (dst, src) in enumerate((("yz", "zo"), ("yl", "out"))):
                    add(dst, "Y", {"Y": ("y", 1)}, lambda e, T, dst=dst, src=src + sb, b=b: [e.dma_start(T[dst][:, 128 * b:128 * b + 128], T[src][:, :])],
                        [src + sb], [], late=2.0, sem="o%d%d" % (k, b))
        if not last:
            for b in (1 - TAIL, TAIL):
                now["b"] = "AB"[b == TAIL]
                of = ("ofm%d" % b, 16, 24)
                VG("put", 128, tc(by(XS, of), P("yi%d" % b)), ["yi%d" % b, of], ["xs"], "sv")
    return ops


def price(kind, n, K):
    cyc = 0.00083 * K["f"]
    return {"v": max(64, n) * cyc + K["vfix"], "s": n * cyc + 0.065, "gv": 0.05 + n * K["gat"] * cyc, "gs": 0.065 + n * K["gat"] * cyc,
            "sv": 0.05 + n * K["sca"] * cyc, "t": n * K["pe"] * K["f"] + 0.03, "g": 0.17 + n * cyc, "y": 0.1 * n, "i": K["issue"], "0": 0.0}[kind]


def link(ops):
    hist = {}
    for k, op in enumerate(ops):
        deps, order = set(), set()
        acc = [(r, False) for r in op["rd"]] + [(w, True) for w in op["wr"]]
        for (bn, a, z), wr in acc:
            ps = SCRATCH[bn][0] == "psum"
            for (a2, z2, k2, w2) in hist.get(bn, []):
                if k2 == k:
                    continue
                over = a < z2 and a2 < z
                same = op["q"] == ops[k2]["q"] and len(op["q"]) == 1 and op["q"] != "Y"
                if ps:
                    if not same:
                        deps.add(k2)
                    elif over and w2 and op["q"] != "T":
                        deps.add(k2)
                    else:
                        order.add(k2)
                elif over and (wr or w2):
                    if w2 or not same:
                        deps.add(k2)
                    else:
                        order.add(k2)
        for (bn, a, z), wr in acc:
            h = hist.setdefault(bn, [])
            if wr and SCRATCH[bn][0] != "psum":
                h[:] = [x for x in h if not (a <= x[0] and x[1] <= z)]
            if SCRATCH[bn][0] == "psum":
                h[:] = [x for x in h if not (x[2] in deps and (ops[x[2]]["q"] != op["q"] or (a <= x[0] and x[1] <= z)))]
            h.append((a, z, k, wr))
        if op.get("after") is not None:
            for k2 in range(k):
                if ops[k2].get("send", (None,))[:2] == op["after"]:
                    order.add(k2)
        op["deps"], op["order"] = deps, order - deps


def ranks(ops, succ, pos, span):
    rank = [op["t"] * span + pos.get(op["name"], 0.0) + k * 1e-6 for k, op in enumerate(ops)]
    for k in range(len(ops) - 1, -1, -1):
        if ops[k]["t"] < 0:
            rank[k] = min(rank[x] for x in succ[k]) - 1e-3
    return rank


def fill(ops, K, pos, span):
    n = len(ops)
    succ = [[] for _ in range(n)]
    left = [0] * n
    for k, op in enumerate(ops):
        for d in op["deps"] | op["order"]:
            succ[d].append(k)
            left[k] += 1
    rank = ranks(ops, succ, pos, span)
    busy = {q: [] for q in "VSTGYE"}
    est, total, lat = [0.0] * n, 0.0, K["lat"]
    ready = [k for k in range(n) if left[k] == 0]
    while ready:
        k = min(ready, key=lambda x: rank[x])
        ready.remove(k)
        op = ops[k]
        best = None
        for q in op["q"]:
            c, s, iv = price(*op["c"][q], K), est[k], busy[q]
            j = len(iv)
            while j and iv[j - 1][1] > s:
                j -= 1
            while j < len(iv) and iv[j][0] < s + c:
                s = max(s, iv[j][1])
                j += 1
            if best is None or s + c < best[0]:
                best = (s + c, s, q, j, c)
        f, s, q, j, c = best
        if q != "E":
            busy[q].insert(j, (s, f))
        op["at"], op["on"], op["cost"] = s, q, c
        f += K.get(op.get("late"), op.get("late")) or 0.0
        total = max(total, f)
        for x in succ[k]:
            left[x] -= 1
            est[x] = max(est[x], f + (lat if k in ops[x]["deps"] else 0.0))
            if left[x] == 0:
                ready.append(x)
    return sorted(range(n), key=lambda k: (ops[k]["at"], k)), total


def issue(ops, pos, span):
    n = len(ops)
    succ = [[] for _ in range(n)]
    left = [0] * n
    for k, op in enumerate(ops):
        for d in op["deps"] | op["order"]:
            succ[d].append(k)
            left[k] += 1
    rank = [op["t"] * span + pos.get(op["name"], -9 * span) for op in ops]
    ready, seq = [k for k in range(n) if left[k] == 0], []
    while ready:
        k = min(ready, key=lambda x: (rank[x], x))
        ready.remove(k)
        seq.append(k)
        for x in succ[k]:
            left[x] -= 1
            if left[x] == 0:
                ready.append(x)
    return seq


PLAN = {}
ORDER = """
V: eiB- kiB- kbB- eaB- ofiB- oflB- yiB- newB- putB- thrB- lqA g10A g13A sc1A sc0A sc2A sc3A hb0A lqB hb1A hb3A hb2A siA sc3B uhA sc0B ulA okA hb3B sc1B puA okmA hb1B hb0B sc2B ciA ofmA ccA gzA ofcA hb2B g20A siB okB uhB ulB okmB puB g22A cmA ciB ofmB ccB gzB ofcB g21B g20B kwA rvA kbA restA oflA newA kiA cmB rvB ofiA restB loA+ loB+ yiA putA kwB
S: rcp3A g13B g10B g11B rcp3B g12B zsA sqA zsB zcA g23A g21A ab0A sqB ab3A ab1A ab2A zcB g23B zoB- g22B ab1B zoA- ab0B ab3B ab2B cnB g11A+ nthB g12A+
T: sub3A- uB- wmB- sub1A- sub2A- ztB- kp0A- kp1A- sub1B- sub0B- sub3B- nokB- sub2B- kp0B- cutB- kp1B- cut2B- rev3A su0A su1A rev3B cnt0A cnt1A lastA su0B uA wmA cnt0B su1B ztA cnt1B sub0A lastB nokA
G: sendA sendB
Y: yzB yzA- ylA sh0A+ sh0B+ sh1A+ cwA+ ylB- sh1B+ cwB+
"""


def issue(ops):
    which = {(op["name"], op["t"]): k for k, op in enumerate(ops)}
    before = [set(op["deps"] | op["order"]) for op in ops]
    for op in ops:
        op["on"] = op["q"]
    for line in ORDER.strip().split("\n"):
        q, names = line.split(":")
        row = [k for k, op in enumerate(ops) if op["t"] < 0 and op["q"] == q]
        for t in range(-1, RO + 1):
            for w in names.split():
                k = which.get((w.strip("+-"), t + w.count("+") - w.count("-")))
                if k is not None and ops[k]["t"] >= 0:
                    row.append(k)
        for j, k in enumerate(row):
            ops[k]["on"] = q
            before[k].update(row[j - 1:j])
    seq, seen = [], set()
    while len(seq) < len(ops):
        go = [k for k in range(len(ops)) if k not in seen and before[k] <= seen]
        assert go
        seq += go
        seen.update(go)
    return seq


def plan():
    if not PLAN:
        ops = build()
        link(ops)
        PLAN["ops"], PLAN["seq"] = ops, issue(ops)
    return PLAN["ops"], PLAN["seq"]


def helper(topo, core, dst):
    for c in topo.cores_of(core):
        if c != core and topo.die(c) == topo.die(core) and topo.may_write(c, dst):
            return c
    return None


def send(g, T, topo, core, dst, out, src, rsem):
    rid, pid = topo.addr(dst, core)
    (ob, o0, o1), (ib, i0, i1) = at(out), at(src)
    g.remote_dma(out_ap=T[ob][:, o0:o1], in_ap=T[ib][:, i0:i1], remote_sem=T.sem[rsem], local_sem=T.sem["lsem"], pid=pid, routing_id=rid, dma_engine_mask=topo.mask(core, dst))
    return len(topo.engines(core, dst))


def rank_program(g, core, T, topo):
    rank = T.rank_of(core)
    if rank is None:
        for r, c in enumerate(T.cores):
            dst = T.cores[(r + HOPS[1]) % N]
            if not topo.may_write(c, dst) and helper(topo, c, dst) == core:
                sent = 0
                for t in range(1, RO):
                    g.wait_ge(T.sem["h%d" % t], len(topo.engines(c, core)))
                    sent += send(g, T, topo, core, dst, "land%d1" % t, "rel%d" % t, "a%d1" % t)
                g.wait_ge(T.sem["lsem"], sent)
        return
    arrive = []
    for hop in HOPS:
        src = T.cores[(rank - hop) % N]
        arrive.append(len(topo.engines(src if topo.may_write(src, core) else helper(topo, src, core), core)))
    ops, seq = plan()
    eng = {"V": g.vector, "S": g.scalar, "T": g.tensor, "G": g, "Y": g.sync}
    semn = {"V": "sV", "S": "sS", "T": "sT", "G": "sG"}
    g.sync.dma_start(T.xs[:, :], T.field[:, :]).then_inc(T.sem["dx"], 16)
    g.scalar.dma_start(T.l0[:, :], T.tube[:, :]).then_inc(T.sem["dt"], 16)
    g.scalar.dma_start(T.wi[:, :], T.wt[:, :]).then_inc(T.sem["dw"], 16)
    g.scalar.dma_start(T.ki[:, :], T.kn[:, :]).then_inc(T.sem["dk"], 16)
    g.scalar.dma_start(T.li[:, :], T.lim[:, :]).then_inc(T.sem["dl"], 16)
    count = {}
    known = {q: {} for q in "VSTGY"}
    done, snap = {}, {}
    sent = 0
    for k in seq:
        op = ops[k]
        q = op["on"]
        if q == "E":
            done[k] = op["fn"] if op["after"] is None else (op["fn"][0], arrive[op["after"][1]])
            snap[k] = {}
            continue
        e = eng[q]
        need = {}
        for d in sorted(op["deps"]):
            if d in done:
                s, v = done[d]
                if known[q].get(s, 0) < v and need.get(s, (0, 0))[0] < v:
                    need[s] = (v, d)
        for s in sorted(need):
            v, d = need[s]
            if any(snap[d2].get(s, 0) >= v for s2, (v2, d2) in need.items() if s2 != s):
                continue
            e.wait_ge(T.sem[s], v)
        for s, (v, d) in need.items():
            kn_ = known[q]
            kn_[s] = max(kn_.get(s, 0), v)
            for s2, v2 in snap[d].items():
                kn_[s2] = max(kn_.get(s2, 0), v2)
        snap[k] = dict(known[q])
        if op.get("send"):
            t, b, nb = op["send"]
            dst = T.cores[(rank + HOPS[b]) % N]
            if topo.may_write(core, dst):
                sent += send(g, T, topo, core, dst, "land%d%d" % (t + 1, b), nb, "a%d%d" % (t + 1, b))
            else:
                sent += send(g, T, topo, core, helper(topo, core, dst), "rel%d" % (t + 1), nb, "h%d" % (t + 1))
            continue
        ins = op["fn"](e, T, q == "S") if op.get("both") else op["fn"](e, T)
        s, n = op.get("sem") or semn[q], 16 if q == "Y" else 1
        for x in ins:
            x.then_inc(T.sem[s], n)
        count[s] = count.get(s, 0) + n * len(ins)
        done[k] = (s, count[s])
    for s in sorted(count):
        g.sync.wait_ge(T.sem[s], count[s])
    g.wait_ge(T.sem["lsem"], sent)
